import numpy as np, ml_dtypes
CORES = [40,64,80,88,96,104,120,144]
N = 8
import mx_ref
BF = ml_dtypes.bfloat16
def gcols(t, e):
    v = np.concatenate([t.reshape(8, 16, -1, 4), np.zeros((8, 16, 1, 4), BF)], axis=2)
    return np.ascontiguousarray(np.stack([v[g][:, e[g]] for g in range(8)])).reshape(128, -1)
def tile(rs):
    return np.stack(rs, axis=2).reshape(128, -1).astype(BF)
def cut(t, i, w=512):
    return t[:, w * i:w * i + w]
def pick(q, e):
    c = np.concatenate([q[0].reshape(128, -1, 4), np.zeros((128, 1, 4), np.uint8)], axis=1); s = np.concatenate([q[1], np.ones((16, 1), np.uint8)], axis=1)
    return (np.ascontiguousarray(c[:, e].reshape(128, -1)), np.ascontiguousarray(s[:, e]))
def join(*qs):
    return (np.concatenate([q[0] for q in qs], axis=1), np.concatenate([q[1] for q in qs], axis=1))
def put(q, e, v):
    c, s = q[0].reshape(128, -1, 4).copy(), q[1].copy(); c[:, e] = v[0].reshape(128, -1, 4); s[:, e] = v[1]
    return (c.reshape(128, -1), s)
def pk(c, s):
    return (np.ascontiguousarray(c), mx_ref.live(s))
def emit(q):
    return q[0], q[1]
def packed(v, rng):
    q = [mx_ref.quantize(np.ascontiguousarray(v[r])) for r in range(N)]
    return np.stack([a for a, b in q]), np.stack([mx_ref.plane(b, rng) for a, b in q])
def values_of_codes():
    e, c = np.zeros((128, 128, 4), np.float32), np.zeros((128, 2, 4), np.uint8)
    e[np.arange(128), np.arange(128), 0] = 1
    c[:127, :, 0] = np.arange(256).reshape(2, 128).T[:127]
    return mx_ref.matmul(mx_ref.quantize(e.reshape(128, 512).astype(BF)), (c.reshape(128, 8), np.full((16, 2), 127, np.uint8))).T.reshape(-1).astype(np.float64)
CODE_VALUE, SCALE_VALUE = values_of_codes(), 2.0 ** (np.arange(256) - 127.0)
def decode(q):
    return (CODE_VALUE[q[0]].reshape(16, 8, -1, 4) * SCALE_VALUE[q[1]][:, None, :, None] + 0.0).reshape(128, -1).astype(np.float32)
def f(rng, *shape):
    return mx_ref.flush((rng.standard_normal(shape, dtype=np.float32) * np.exp2(rng.integers(-2, 3, shape[:-1] + (1,)))).astype(BF))
def wide(rng, *shape, cols=0):
    v = rng.standard_normal(shape, dtype=np.float32) * np.exp2(rng.integers(-12, 13, shape)).astype(np.float32)
    if cols: v *= np.repeat(np.exp2(rng.integers(-cols, cols + 1, shape[:-2] + (1, shape[-1] // 4))) * (rng.random(shape[:-2] + (1, shape[-1] // 4)) > 0.0625), 4, axis=-1).astype(np.float32)
    return mx_ref.flush(v.astype(BF))
C = 416
def order(p):
    return np.argsort(-(p[::16] + np.float32(0.0)), axis=1, kind="stable")
def swap(qs, k, n):
    e = np.arange(1, n, 2)
    return [put(qs[r], e, pick(qs[r ^ k], e)) for r in range(N)]
def half(z):
    return mx_ref.quantize(np.ascontiguousarray((z * np.float32(0.5)).astype(BF).reshape(128, -1)))
def big(v, k):
    v = v.astype(np.float32) * np.float32(k)
    v[np.abs(v) < np.float32(2.0 ** -16)] = 0
    return v.astype(BF)
def numbers_of(rng):
    return {"x": big(f(rng, N, 128, 4 * C), 1), "ua": np.array(f(rng, N, 128, 512)), "ub": np.array(f(rng, N, 128, 512)), "v": np.array(f(rng, N, 128, 512))}
def weights(rng, w):
    c, p = packed(w, rng)
    return {"wc": c, "ws": p}
def still(rng):
    w = np.zeros((N, 128, 4, 128, 4), np.float32)
    i = np.arange(128)
    for b in range(4): w[:, i, b, i, b] = 32
    return weights(rng, w.reshape(N, 128, 2048).astype(BF))
def signs(rng):
    return np.stack([rng.permutation(8) % 2 * 2.0 - 1.0 for r in range(N)])
def setup_inputs(rng):
    return {**numbers_of(rng), **weights(rng, f(rng, N, 128, 2048))}
def setup_inputs_ties(rng):
    d = numbers_of(rng)
    e = rng.permutation(N)
    x = d["x"].reshape(N, 8, 16, C, 4)
    for r in range(N):
        k = np.zeros(C, int) if r == e[0] else rng.permutation(C) % 3
        a = x[r][:, :8, :3].copy()
        a[:, :, 2] = 0
        x[r][:, :8] = a[:, :, k]
    x[e[1]] = 0
    for n in ("ua", "ub"):
        u = d[n].reshape(N, 8, 16, 128, 4)
        u[:, :, 8:, ::16] = 0
        d[n] = u.reshape(N, 128, 512)
    w = np.array(f(rng, N, 128, 2048)).reshape(N, 8, 16, 4, 8, 16, 4)
    w[:, :, 8:, :, :, :8] = 0
    return {**d, "x": x.reshape(N, 128, 4 * C), **weights(rng, w.reshape(N, 128, 2048))}
def setup_inputs_near(rng):
    d = numbers_of(rng)
    x = np.zeros((N, 8, 16, C, 4), np.float32)
    m = np.arange(C) // 2
    x[:, :, 0, :, 0] = np.repeat(signs(rng)[::2], 2, axis=0)[:, :, None]
    for p, s in ((8, m), (10, (C // 2 - 1 - m) // 2)):
        g = ((s[:, None] >> np.arange(8)) & 1) * np.exp2(np.arange(8) - 23.0)
        x[:, :, p] = g[:, :4]
        x[:, :, p + 1] = g[:, 4:]
    x[:, :, 12:] = rng.integers(4, 8, (N, 8, 4, C, 4)) * rng.choice([-1.0, 1.0], (N, 8, 4, C, 4)) * 2.0 ** -20
    for n, p in (("ua", 8), ("ub", 10)):
        u = d[n].reshape(N, 128, 128, 4)
        u[:, :, ::16] = 0
        for h in range(0, 128, 16):
            u[:, h, h, 0] = 2.0 ** -28
            u[:, h + p:h + p + 2, h] = 2.0 ** -28
        d[n] = u.reshape(N, 128, 512)
    return {**d, "x": x.reshape(N, 128, 4 * C).astype(BF), **still(rng)}
def setup_inputs_huge(rng):
    d = numbers_of(rng)
    x = 2.0 ** 29 * (0.6 + 0.4 * rng.random((N, 128, C, 4)))
    both = np.repeat(rng.permutation(N // 2) < N // 4, 2)
    c = np.stack([rng.permutation(C) % 2 * 2.0 - 1.0 for r in range(N)])
    c[~both] = 1
    x *= c[:, None, :, None]
    g = signs(rng)
    g[both] = g[both][:, :1]
    for n, s in (("ua", g), ("ub", signs(rng))):
        u = d[n].reshape(N, 128, 128, 4)
        a = 2.0 ** 30 * (1 - 0.25 * rng.random((N, 128, 8, 4))) * s[:, None, :, None]
        u[:, :, ::16] = a.astype(np.float32).astype(BF)
        d[n] = u.reshape(N, 128, 512)
    return {**d, "x": x.astype(np.float32).reshape(N, 128, 4 * C).astype(BF), **still(rng)}
def setup_inputs_sizes(rng):
    d = setup_inputs(rng)
    k = np.concatenate([rng.permutation(4) for i in range(N // 4)]) * 5.0
    d["x"] = big(d["x"].astype(np.float32) * np.exp2(k).astype(np.float32)[:, None, None], 1)
    return d
def setup_inputs_spread(rng):
    d = setup_inputs(rng)
    d["x"] = big(wide(rng, N, 128, 4 * C, cols=6), 1)
    return d
def check_inputs(d):
    b = []
    for k in ("x", "ua", "ub", "v"):
        a = np.abs(d[k].astype(np.float32))
        if not (np.isfinite(a).all() and ((a == 0) | (a >= 2.0 ** -30) & (a <= 2.0 ** 30)).all()): b.append("a value of " + k)
    return b
def reference(x, ua, ub, v, wc, ws):
    lay = [pk(wc[r], ws[r]) for r in range(N)]
    now = [mx_ref.quantize(x[r]) for r in range(N)]
    orders, highs = [], []
    for l in range(2):
        s, n = (ua, ub)[l], C >> l
        d = decode(join(*now)).astype(BF)
        o, low, high = [], [], []
        for r in range(N):
            o.append(order(mx_ref.matmul(mx_ref.quantize(s[r]), now[r])))
            z = gcols(cut(d, r, 4 * n), o[r]).astype(np.float32).reshape(128, n // 2, 2, 4)
            low.append(half(z[:, :, 0] + z[:, :, 1]))
            high.append(half(z[:, :, 0] - z[:, :, 1]))
        orders.append(o)
        highs.append(high)
        low = swap(low, 1 << l, n // 2)
        now = [mx_ref.quantize(tile([mx_ref.matmul(pick(lay[r], np.arange(128 * b, 128 * b + 128)), low[r]) * np.float32(0.03125) for b in range(4)])) for r in range(N)]
    for l in (1, 0):
        m = C >> (l + 1)
        now = swap(now, 1 << l, m)
        d = decode(join(*now, *highs[l]))
        new = []
        for r in range(N):
            a, h = cut(d, r, 4 * m), cut(d, N + r, 4 * m)
            i = np.argsort(orders[l][r], axis=1)
            new.append(mx_ref.quantize(gcols(np.concatenate([(a + h).astype(BF), (a - h).astype(BF)], axis=1), i // 2 + m * (i % 2))))
        now = new
    y, ol = np.zeros((N, 128, C), np.float32), np.zeros((N, 8, C + C // 2), np.float32)
    oc, osc = np.zeros((N, 128, 4 * C), np.uint8), np.zeros((N, 16, C), np.uint8)
    for r in range(N):
        y[r] = mx_ref.matmul(mx_ref.quantize(v[r]), now[r])
        ol[r] = np.concatenate([orders[0][r], orders[1][r]], axis=1)
        oc[r], osc[r] = emit(now[r])
    return {"y": y, "ol": ol, "oc": oc, "osc": osc}

@@ -1,0 +1,709 @@
+import numpy as np
+from concourse.bass import DstId, RemoteDMATransfer
+from concourse.mybir import dt, AluOpType, ActivationFunctionType
+
+ALU = AluOpType
+ACT = ActivationFunctionType
+C = 416
+BIG = 2.0e29
+ON_VECTOR = ((4, 5), (1, 2))
+ROWS = (2, 2)
+CUTS = ((0, 5, 8, 10, 13), (0, 3, 5, 7))
+X4, U8, BF, F32, I32, U16 = "float8_e4m3fn_x4", "uint8", "bfloat16", "float32", "int32", "uint16"
+
+SCRATCH = {}
+
+
+def _buf(name, n, dtype):
+    SCRATCH[name] = ("sbuf", [128, n], dtype)
+
+
+def _mx(name, n):
+    _buf(name + "c", n, X4)
+    _buf(name + "s", n, U8)
+
+
+for _n, _w in (("xt", 4 * C), ("uat", 512), ("ubt", 512), ("vt", 512), ("et", 2048), ("ones", 128),
+               ("ident", 128), ("jv", C), ("rz0", 8 * 160), ("rz1", 5 * 224), ("z0", 2 * 8 * C), ("z1", 2 * 5 * 224),
+               ("zs", 2 * 8 * C), ("sg", 4800), ("jk", 14 * 96), ("tt", 2 * C), ("o0", 896), ("o1", 512), ("to", 1024),
+               ("dw0", 4 * C), ("dw1", 4 * 208), ("g0", 8 * 112), ("g1", 8 * 64), ("lot", 512), ("let", 512),
+               ("ht0", 4 * 224), ("ht1", 512), ("at1", 4 * 224), ("ret", 512), ("rot", 512), ("hw0", 4 * C),
+               ("hm", 4 * 208), ("hs0", 2 * C), ("ab1", 4 * C), ("ab0", 2 * C), ("da0", 2 * 208), ("u1t", 4 * 208),
+               ("u0t", 4 * C)):
+    _buf(_n, _w, BF)
+for _n, _w in (("i32f", 224), ("tm", 2 * C), ("cum", 1056), ("rsa", 32), ("rsb0", 32), ("rsb1", 32), ("rsc", 96),
+               ("rk", 32), ("xp", 64), ("wt", 96), ("wl", 32), ("cf", 16), ("olf", C + C // 2), ("yt", C)):
+    _buf(_n, _w, F32)
+for _n, _w in (("ci", 52), ("rw0", 28), ("rw1", 16), ("pa", 64), ("la", 160), ("lb", 160), ("lst", 16), ("rl", 16)):
+    _buf(_n, _w, I32)
+for _n, _w in (("uof", 16), ("pos", 28), ("ll0", 32), ("ll1", 32), ("olo", 28), ("ua0", 28), ("uh0", 28), ("uh1", 14)):
+    _buf(_n, _w, U16)
+for _n, _w in (("qx", C), ("qa", 128), ("qb", 128), ("qv", 128), ("pa_", 256), ("pb_", 256), ("qe", 512), ("qw", 512),
+               ("s0", 208), ("s1", 208), ("s2", 208), ("mid0", 240), ("mid1", 192), ("qa1", 224), ("qh0", 224),
+               ("qh1", 240), ("up1", 288), ("qu1", 208), ("qu0", C)):
+    _mx(_n, _w)
+for _n, _w, _v in (("r0", 52, 208), ("r1", 52, 208), ("r2", 52, 208), ("rh", 104, 104), ("re_", 52, 52)):
+    _buf(_n + "c", _w, X4)
+    _buf(_n + "s", _v, U8)
+for _k in range(8):
+    SCRATCH["ps%d" % _k] = ("psum", [128, 512], F32)
+
+NDMA = 24
+SEMAPHORES = (["cV", "cA", "cP", "cG", "sent", "a0", "a1", "a2", "a3", "ah", "ae", "al", "h0", "h1", "h2", "hh", "he",
+               "hl"] + ["d%d" % _k for _k in range(NDMA)])
+
+
+def bits(engines):
+    m = 0
+    for e in engines:
+        m |= 1 << e
+    return m
+
+
+def helpers(core, far, topo):
+    ok = [c for c in topo.cores_of(core) if c != core and topo.may_write(c, far)]
+    near = [c for c in ok if topo.die(c) == topo.die(core)]
+    other = [c for c in ok if topo.die(c) != topo.die(core)]
+    return near[0], near[1], other[0], other[1]
+
+
+def pieces(nb, dd):
+    out = []
+    for b in range(nb):
+        lo, hi = b + 1, b + dd + 1
+        if hi <= nb:
+            out.append([b, lo, hi, False, 0])
+        elif lo >= nb:
+            out.append([b, 0, hi - nb, True, 0])
+        else:
+            out.append([b, lo, nb, False, 0])
+            out.append([b, 0, hi - nb, True, 1])
+    ends = [0] * dd
+    for p in sorted(out, key=lambda p: p[1]):
+        s = ends.index(p[1])
+        ends[s] = p[2]
+        p.append(s + 2)
+    return out
+
+
+def relay_program(g, core, T, topo, r):
+    me = T.cores[r]
+    p1, p2 = T.cores[r ^ 1], T.cores[r ^ 2]
+    ha, hb, hc, hd = helpers(me, p1, topo)
+    quarter = len(topo.engines(me, core)) // 4
+    total = [0]
+
+    def on(dst, out, in_, sem):
+        rid, pid = topo.addr(dst, core)
+        e = topo.engines(core, dst)
+        g.remote_dma(out, in_, T.sem[sem], T.sem.sent, pid, rid, bits(e))
+        total[0] += len(e)
+
+    def cod(name, a, b):
+        return T[name][:, a:b].bitcast(dt.uint8)
+
+    if core == ha:
+        g.wait_ge(T.sem.h0, quarter)
+        on(p1, cod("mid0c", 8, 60), cod("r0c", 0, 52), "a0")
+        g.wait_ge(T.sem.h1, 2 * quarter)
+        on(p2, cod("mid1c", 12, 64), cod("r1c", 0, 52), "a1")
+        g.wait_ge(T.sem.h2, 2 * quarter)
+        on(p2, cod("up1c", 4, 56), cod("r2c", 0, 52), "a2")
+    elif core == hb:
+        g.wait_ge(T.sem.h0, quarter)
+        on(p1, T.mid0s[:, 8:112], T.r0s[:, 0:104], "a0")
+        g.wait_ge(T.sem.h1, 2 * quarter)
+        on(p2, T.mid1s[:, 12:64], T.r1s[:, 0:52], "a1")
+        g.wait_ge(T.sem.h2, 2 * quarter)
+        on(p2, T.up1s[:, 4:56], T.r2s[:, 0:52], "a2")
+    elif core == hc:
+        g.wait_ge(T.sem.h0, quarter)
+        on(p1, cod("mid0c", 60, 112), cod("r0c", 0, 52), "a0")
+        g.wait_ge(T.sem.hh, 2 * quarter)
+        on(p1, T.qh1s[:, 8:112], T.rhs[:, 0:104], "ah")
+        g.wait_ge(T.sem.he, 2 * quarter)
+        on(p1, cod("up1c", 108, 160), cod("re_c", 0, 52), "ae")
+    elif core == hd:
+        g.wait_ge(T.sem.hl, quarter)
+        on(p1, T.lst[:, 0:13], T.rl[:, 0:13], "al")
+        g.wait_ge(T.sem.hh, 2 * quarter)
+        on(p1, cod("qh1c", 8, 112), cod("rhc", 0, 104), "ah")
+        g.wait_ge(T.sem.he, 2 * quarter)
+        on(p1, T.up1s[:, 108:160], T.re_s[:, 0:52], "ae")
+    if total[0]:
+        g.wait_ge(T.sem.sent, total[0])
+
+
+def rank_program(g, core, T, topo):
+    rank = T.rank_of(core)
+    if rank is None:
+        for r, c in enumerate(T.cores):
+            if core in topo.cores_of(c):
+                relay_program(g, core, T, topo, r)
+        return
+    p1, p3 = T.cores[rank ^ 1], T.cores[rank ^ 3]
+    ha, hb, hc, hd = helpers(core, p1, topo)
+
+    queue = {"V": g.vector, "A": g.scalar, "P": g.tensor, "G": g, "S": g.sync}
+    clock = {q: {} for q in queue}
+    count = {}
+    toks = [None]
+    wr, rd = {}, {}
+
+    def cols(v):
+        return slice(v[1], v[2], v[3])
+
+    def state(name):
+        if name not in wr:
+            n = SCRATCH[name][1][1]
+            wr[name] = np.zeros(n, np.int64)
+            rd[name] = {}
+        return wr[name], rd[name]
+
+    def wait(q, tid):
+        sem, n, seen = toks[tid]
+        if clock[q].get(sem, 0) >= n:
+            return
+        queue[q].wait_ge(T.sem[sem], n)
+        for s, k in seen.items():
+            if clock[q].get(s, 0) < k:
+                clock[q][s] = k
+        clock[q][sem] = n
+
+    def before(q, reads, writes):
+        need = set()
+        for v in reads:
+            w, r = state(v[0])
+            bank = v[0].startswith("ps")
+            need.update(np.unique(w if bank else w[cols(v)]).tolist())
+            if bank:
+                for who, a in r.items():
+                    if who != q:
+                        need.update(np.unique(a).tolist())
+        for v in writes:
+            w, r = state(v[0])
+            s = slice(None) if v[0].startswith("ps") else cols(v)
+            need.update(np.unique(w[s]).tolist())
+            for a in r.values():
+                need.update(np.unique(a[s]).tolist())
+        need.discard(0)
+        for tid in sorted(need, reverse=True):
+            wait(q, tid)
+
+    def after(who, tok, reads, writes):
+        toks.append(tok)
+        tid = len(toks) - 1
+        for v in reads:
+            w, r = state(v[0])
+            if who not in r:
+                r[who] = np.zeros(len(w), np.int64)
+            r[who][cols(v)] = tid
+        for v in writes:
+            state(v[0])[0][cols(v)] = tid
+        return tid
+
+    def run(q, reads, writes, call):
+        before(q, reads, writes)
+        sem = "c" + q
+        count[sem] = count.get(sem, 0) + 1
+        call().then_inc(T.sem[sem], 1)
+        return after(q, (sem, count[sem], dict(clock[q])), reads, writes)
+
+    ndma = [0]
+
+    def dma(q, out, in_, reads, writes):
+        before(q, reads, writes)
+        sem = "d%d" % ndma[0]
+        ndma[0] += 1
+        count[sem] = 16
+        queue[q].dma_start(out, in_).then_inc(T.sem[sem], 16)
+        return after(sem, (sem, 16, dict(clock[q])), reads, writes)
+
+    def lands(sem, n, writes):
+        count[sem] = n
+        after(sem, (sem, n, {}), [], writes)
+
+    def V(name, a=0, b=None, s=1):
+        return (name, a, SCRATCH[name][1][1] if b is None else b, s)
+
+    def col(name, a):
+        return (name, a, a + 1, 1)
+
+    def ap(v):
+        if not isinstance(v, tuple):
+            return v
+        if len(v) == 2:
+            return ap(v[0]).indirect(ap(v[1]))
+        if v[3] == 1:
+            return T[v[0]][:, v[1]:v[2]]
+        return T[v[0]][:, v[1]:v[2]:v[3]]
+
+    def named(*vs):
+        out = []
+        for v in vs:
+            if isinstance(v, tuple):
+                out.extend(v if len(v) == 2 else [v])
+        return out
+
+    def tcopy(out, in_):
+        if len(out) == 2:
+            return run("V", named(in_, out[1]), [out[0]], lambda: g.vector.tensor_copy(ap(out), ap(in_)))
+        return run("V", named(in_), [out], lambda: g.vector.tensor_copy(ap(out), ap(in_)))
+
+    def tt(out, a, b, op):
+        return run("V", named(a, b), [out], lambda: g.vector.tensor_tensor(ap(out), ap(a), ap(b), op))
+
+    def ts(out, a, s1, op0, s2=None, op1=None):
+        if op1 is None:
+            return run("V", named(a, s1), [out], lambda: g.vector.tensor_scalar(ap(out), ap(a), ap(s1), None, op0))
+        return run("V", named(a, s1, s2), [out],
+                   lambda: g.vector.tensor_scalar(ap(out), ap(a), ap(s1), ap(s2), op0, op1))
+
+    def scan(out, a, b, op0, op1, first=0.0):
+        return run("V", named(a, b, first), [out],
+                   lambda: g.vector.tensor_tensor_scan(ap(out), ap(a), ap(b), ap(first), op0, op1))
+
+    def turn(out, a):
+        return run("V", [a], [out], lambda: g.vector.transpose(ap(out), ap(a)))
+
+    def fill(out, c):
+        return run("V", [], [out], lambda: g.vector.memset(ap(out), c))
+
+    def act(out, a, func, bias=None, scale=None, accum=None):
+        kw = {}
+        if bias is not None:
+            kw["bias"] = ap(bias)
+        if scale is not None:
+            kw["scale"] = scale
+        if accum is not None:
+            kw["accum_out"] = ap(accum)
+        return run("A", named(a, bias), named(out, accum), lambda: g.scalar.activation(ap(out), ap(a), func, **kw))
+
+    def iota(out, pattern, base=0, cm=0):
+        if SCRATCH[out[0]][2] == I32:
+            return run("G", [], [out], lambda: g.iota(ap(out), pattern, base, cm))
+        return run("G", [], [out], lambda: g.iota(ap(out), pattern, base, cm, allow_small_or_imprecise_dtypes=True))
+
+    def const(out, c=0):
+        return iota(out, [[0, len(range(out[1], out[2], out[3]))]], c)
+
+    def quant(name, a, tile, t0, n):
+        c, s, t = V(name + "c", a, a + n), V(name + "s", a, a + n), V(tile, 4 * t0, 4 * (t0 + n))
+        return run("V", [t], [c, s], lambda: g.vector.quantize_mx(ap(c), ap(s), ap(t)))
+
+    def mm(bank, w, w0, x, x0, n):
+        vs = [V(w + "c", w0, w0 + 128), V(w + "s", w0, w0 + 128), V(x + "c", x0, x0 + n), V(x + "s", x0, x0 + n)]
+        out = V("ps%d" % bank, 0, n)
+        return run("P", vs, [out],
+                   lambda: g.tensor.matmul_mx(ap(out), ap(vs[0]), ap(vs[1]), ap(vs[2]), ap(vs[3]), True, True))
+
+    def ps(bank, a, b):
+        return V("ps%d" % bank, a, b)
+
+    def u8(v):
+        return ap(v).bitcast(dt.uint8) if SCRATCH[v[0]][2] == X4 else ap(v)
+
+    count["sent"] = 0
+
+    def send(items):
+        before("G", [it[2] for it in items], [])
+        if len(items) == 1:
+            dst, out, in_, sem, e = items[0]
+            rid, pid = topo.addr(dst, core)
+            g.remote_dma(u8(out), u8(in_), T.sem[sem], T.sem.sent, pid, rid, bits(e))
+        else:
+            trs = []
+            for dst, out, in_, sem, e in items:
+                rid, pid = topo.addr(dst, core)
+                trs.append(RemoteDMATransfer(dst_ids=[DstId(rid=rid, pnc=pid)], dma_engine_mask=bits(e),
+                                             remote_sem=T.sem[sem], src=u8(in_), dst=u8(out)))
+            g.remote_dma_fused(trs, local_sem=T.sem.sent)
+        count["sent"] += sum(len(it[4]) for it in items)
+
+    eng = topo.engines(core, ha)
+    q4 = len(eng) // 4
+    off = topo.engines(core, p3)
+    nfar = len(topo.engines(ha, p1))
+
+    def swap_wide(src, land, sem):
+        send([(ha, V(land + "c"), V(src + "c", 0, 52), sem, eng[q4:2 * q4]),
+              (hc, V(land + "c"), V(src + "c", 52, 104), sem, eng[2 * q4:3 * q4]),
+              (hb, V(land + "s"), V(src + "s"), sem, eng[3 * q4:])])
+
+    def swap_narrow(src, land, sem):
+        send([(ha, V(land + "c"), V(src + "c", 0, 52), sem, eng[:2 * q4]),
+              (hb, V(land + "s"), V(src + "s"), sem, eng[2 * q4:])])
+
+    def send2(dst, dst2, src, a, land, m, sem):
+        send([(dst, V(land + "c"), V(src + "c", a, a + m), sem, eng[2 * q4:])])
+        send([(dst2, V(land + "s"), V(src + "s", a, a + m), sem, eng[:2 * q4])])
+
+    def mxv(name, a, b):
+        return [V(name + "c", a, b), V(name + "s", a, b)]
+
+    lands("a0", 3 * nfar, mxv("mid0", 8, 112))
+    lands("a1", 2 * nfar, mxv("mid1", 12, 64))
+    lands("a2", 2 * nfar, mxv("up1", 4, 56))
+    lands("a3", len(off), mxv("up1", 56, 108))
+    lands("ae", 2 * nfar, mxv("up1", 108, 160))
+    lands("ah", 2 * nfar, mxv("qh1", 8, 112))
+    lands("al", nfar, [V("lst", 0, 13)])
+
+    dma("A", T.uat[:], T.ua[:], [], [V("uat")])
+    dma("S", T.xt[:, 0:832], T.x[:, 0:832], [], [V("xt", 0, 832)])
+    dma("S", T.xt[:, 832:1664], T.x[:, 832:1664], [], [V("xt", 832, 1664)])
+    iota(col("ci", 0), [[0, 1]], 0, 1)
+    iota(V("ci", 8, 24), [[16, 2], [32, 4], [0, 2]])
+    const(V("ones"), 1)
+    run("G", [V("ones")], [V("ident")],
+        lambda: g.affine_select(ap(V("ident")), ap(V("ones")), [[-1, 128]], ALU.is_equal, 0.0, 0, 1))
+    iota(V("i32f"), [[0, 7], [1, 32]])
+    fill(V("et"), 0.0)
+    ts(col("ci", 1), col("ci", 0), 31, ALU.bitwise_and)
+    ts(col("ci", 2), col("ci", 0), 4, ALU.arith_shift_right, 1, ALU.bitwise_and)
+    ts(col("ci", 3), col("ci", 0), 1, ALU.bitwise_and)
+    ts(col("ci", 4), col("ci", 0), 15, ALU.bitwise_and)
+    tcopy(V("uof"), V("ci", 8, 24))
+    fill(V("cum", 31, None, 32), 0.0)
+    fill(V("xp"), 0.0)
+    tcopy(V("cf", 0, 4), V("ci", 1, 5))
+    PM32, ODDG, ODDP, P16, EVENG, G64, GBIG, EVENP, CA1, CA2 = [col("cf", i) for i in range(10)]
+
+    def scorer(q, tile, p):
+        quant(q, 0, tile, 0, 128)
+        src, dst, lst = V(q + "c"), V(p + "c"), V("uof")
+        run("V", [src, lst], [dst], lambda: g.vector.tensor_copy(
+            ap(dst).bitcast(dt.uint32), ap(src).bitcast(dt.uint32).indirect(ap(lst))))
+        act(V(p + "s"), (V(q + "s"), lst), ACT.Copy)
+
+    for b in range(4):
+        act(V("et", 512 * b + b, 512 * b + 512, 4), V("ident"), ACT.Copy)
+    quant("qe", 0, "et", 0, 512)
+    ts(V("rz0", 1, None, 8), V("i32f", 0, 160), PM32, ALU.is_gt)
+    for s in range(2, 5):
+        act(V("rz0", s, None, 8), V("et", 0, 160), ACT.Identity, bias=1.0, scale=0.0)
+    scorer("qa", "uat", "pa_")
+    for s in range(5, 8):
+        act(V("rz0", s, None, 8), V("et", 0, 160), ACT.Identity, bias=1.0, scale=0.0)
+    act(EVENG, ODDG, ACT.Identity, bias=1.0, scale=-1.0)
+    act(G64, ODDG, ACT.Copy, scale=64.0)
+    act(GBIG, ODDG, ACT.Copy, scale=BIG)
+    act(EVENP, ODDP, ACT.Identity, bias=1.0, scale=-1.0)
+    act(CA1, ODDP, ACT.Identity, bias=156.0, scale=-52.0)
+    act(CA2, ODDP, ACT.Identity, bias=-156.0, scale=104.0)
+    const(V("rsa"))
+    const(V("rsb0"))
+    const(V("z0", 1, None, 8))
+    const(V("rz0", 0, None, 8))
+    iota(V("jv"), [[1, C]], -(C // 2))
+    const(V("o0"))
+    const(V("to", 0, None, 16))
+    const(V("lot", 448, 512))
+    const(V("let", 448, 512))
+    const(V("at1", 832, 896))
+    const(V("z1", 1, 1040, 5))
+    const(V("z1", 1040, 1120))
+    const(V("z1", 1121, 2160, 5))
+    const(V("z1", 2160, 2240))
+    const(V("rsb1"))
+    const(V("rsb1", 0, 3), -16)
+    const(V("rsb1", 16, 19), -16)
+    const(V("o1"))
+    iota(V("ci", 24, 52), [[128, 7], [16, 4]])
+    quant("qx", 0, "xt", 0, 208)
+    quant("qx", 208, "xt", 208, 208)
+    before("S", [V("xt")], [])
+    dma("S", T.ubt[:], T.ub[:], [], [V("ubt")])
+    dma("S", T.qwc[:].bitcast(dt.uint8), T.wc[:], [], [V("qwc")])
+    dma("S", T.qws[:], T.ws[:], [], [V("qws")])
+    dma("S", T.vt[:], T.v[:], [], [V("vt")])
+    quant("s0", 80, "et", 0, 128)
+
+    def orders(l, state_, scorer_):
+        on_vector, cuts = ON_VECTOR[l], CUTS[l]
+        n = C >> l
+        nb = (n + 31) // 32
+        w, dd = 32 * nb, nb // 2
+        S = dd + 2
+        mid = (nb + 1) // 2
+        z, rz, rsb, dw = "z%d" % l, "rz%d" % l, "rsb%d" % l, "dw%d" % l
+        mm(0, scorer_, 0, state_, 0, w)
+        mm(2, scorer_, 0, state_, 0, w)
+        mm(1, scorer_, 128, state_, 0, w)
+        mm(3, scorer_, 128, state_, 0, w)
+        for b in range(4):
+            mm(4 + b, "qe", 128 * b, state_, 0, n)
+
+        def zv(e, s, k0, k1):
+            return V(z, e * w * S + k0 * S + s, e * w * S + k1 * S, S)
+
+        def scal(e, b):
+            return col("tm", e * w + 32 * b) if 32 * b + 32 <= n else col("cf", 10 + e)
+
+        def diagonal(e):
+            if n < w:
+                ts(scal(e, nb - 1), col("tm", e * w + w - 32), GBIG, ALU.add)
+            tt(zv(e, 0, 0, w), ps(e, 0, w), V("tm", e * w, e * w + w), ALU.is_gt)
+
+        turn(V("tm", 32 * mid, w), ps(0, 32 * mid, w))
+        turn(V("tm", 0, 32 * mid), ps(0, 0, 32 * mid))
+        if n < w:
+            diagonal(0)
+        turn(V("tm", w, 2 * w), ps(1, 0, w))
+        if n == w:
+            diagonal(0)
+        diagonal(1)
+        pcs = pieces(nb, dd)
+        later, at = [], [0]
+        for e in range(2):
+            mine = [p for p in pcs if p[0] >= on_vector[e]]
+            for b, lo, hi, wrapped, second, s in sorted(mine, key=lambda p: p[1]):
+                k0, k1 = 32 * lo, min(32 * hi, n)
+                sg = V("sg", at[0], at[0] + k1 - k0)
+                at[0] += k1 - k0
+                act(sg, ps(2 + e, k0, k1), ACT.Sign, bias=scal(e, b), scale=-1.0)
+                if later:
+                    act(*later.pop())
+                acc = col(rsb if second else "rsa", 16 * e + b)
+                if wrapped:
+                    later.append((zv(e, s, k0, k1), sg, ACT.Sign, 1.0, -1.0, acc))
+                else:
+                    later.append((zv(e, s, k0, k1), sg, ACT.Relu, None, -1.0, acc))
+        act(*later.pop())
+        hl = 16 * dd
+        for e in range(2):
+            for b, lo, hi, wrapped, second, s in pcs[:on_vector[e]]:
+                ts(zv(e, s, 32 * lo, 32 * hi), ps(e, 32 * lo, 32 * hi), scal(e, b), ALU.is_gt)
+        keep = (on_vector[0], on_vector[1] - ROWS[l])
+        for b, lo, hi, wrapped, second, s in pcs[keep[1]:on_vector[1]]:
+            act(V("sg", at[0], at[0] + 2 * hl), zv(1, s, 32 * lo, 32 * hi), ACT.Identity, accum=col("rsa", 16 + b))
+            at[0] += 2 * hl
+        for b in range(4):
+            act(V(dw, n * b, n * b + n), ps(4 + b, 0, n), ACT.Copy, scale=0.5)
+        for e in range(2):
+            for b, lo, hi, wrapped, second, s in pcs[:keep[e]]:
+                j = (7 * e + b) * hl
+                scan(V("jk", j, j + hl), zv(e, s, 32 * lo, 32 * lo + hl), zv(e, s, 32 * lo + hl, 32 * hi), ALU.add,
+                     ALU.add)
+        for e in range(2):
+            if keep[e]:
+                tcopy(V("rsa", 16 * e, 16 * e + keep[e]), V("jk", 7 * e * hl + hl - 1, (7 * e + keep[e]) * hl, hl))
+
+        def columns(e, u0, u1):
+            a, b = (e * w + 32 * u0) * S, (e * w + 32 * u1) * S
+            r = 32 * u0 * S if n < w else 0
+            scan(V("zs", a, b), V(rz, r, r + b - a), V(z, a, b), ALU.mult, ALU.add)
+
+        def flip(e, u0, u1):
+            a, b = e * w + 32 * u0, e * w + 32 * u1
+            turn(V("tt", a, b), V("zs", a * S + S - 1, b * S, S))
+
+        def fold(e, u0, u1):
+            a, b, c = e * w + 32 * u0, e * w + 32 * u1, 512 * e + 32 + 32 * u0
+            scan(V("cum", c, c + b - a), V("zs", a * S + 1, b * S, S), V("tt", a, b), ALU.add, ALU.subtract,
+                 col("cum", c - 1) if u0 else 0.0)
+
+        for i in range(len(cuts) - 1):
+            columns(0, cuts[i], cuts[i + 1])
+        flip(0, 0, nb)
+        columns(1, cuts[0], cuts[1])
+        fold(0, 0, nb)
+        for i in range(1, len(cuts) - 2):
+            columns(1, cuts[i], cuts[i + 1])
+        last = cuts[-2]
+        flip(1, 0, last)
+        columns(1, last, nb)
+        fold(1, 0, last)
+        flip(1, last, nb)
+        tt(V("rsc", 0, 32), V("rsa"), V(rsb), ALU.add)
+        fold(1, last, nb)
+        ts(V("rsc", 32, 64), V("rsc", 0, 32), PM32, ALU.add, float(32 * dd), ALU.add)
+        tt(V("rsc", 64, 96), V("cum", 63, 1056, 32), V("cum", 31, 1024, 32), ALU.subtract)
+        tt(V("rk"), V("rsc", 64, 96), V("rsc", 32, 64), ALU.add)
+        rw, o = "rw%d" % l, "o%d" % l
+        turn(V("xp", 16, 48), V("rk"))
+        ts(V("wt", 64, 80), V("rk", 0, 16), EVENG, ALU.mult)
+        turn(V("wt", 0, 64), V("xp"))
+        ts(V("wt", 80, 96), V("rk", 16, 32), ODDG, ALU.mult)
+        tt(V(rw, 0, 2 * nb, 2), V("wt", 64, 64 + nb), V("wt", 16, 16 + nb), ALU.add)
+        tt(V(rw, 1, 2 * nb, 2), V("wt", 80, 80 + nb), V("wt", 32, 32 + nb), ALU.add)
+        t = n // 16
+        ts(V("pa", 0, t), V(rw, 0, t), 448, ALU.bitwise_and)
+        tt(V("pa", 32, 32 + t), V("pa", 0, t), V(rw, 0, t), ALU.add)
+        ts(V("pos", 0, t), V("pa", 32, 32 + t), G64, ALU.add)
+        j0 = C // 2 - n // 2
+        tcopy((V(o), V("pos", 0, t)), V("jv", j0, j0 + n))
+
+    def lists(l, runs):
+        o, n = "o%d" % l, C >> l
+        wo = SCRATCH[o][1][1]
+        for s0, s1 in runs:
+            for s in range(s0, s1):
+                turn(V("to", 256 * s, 256 * s + wo // 4), V(o, s, wo, 4))
+            a, b = 256 * s0, 256 * s1
+            tt(V("wl", 8 * s0, 8 * s1), V("to", a, b, 32), V("to", a + 16, b, 32), ALU.add)
+            ts(V("ll%d" % l, 8 * s0, 8 * s1), V("wl", 8 * s0, 8 * s1), float(n // 2), ALU.add)
+
+    def fetch(l, odd):
+        n, k = C >> l, (7, 4)[l]
+        for b in range(4):
+            act(V("g%d" % l, 16 * k * (4 * odd + b), 16 * k * (4 * odd + b + 1)),
+                (V("dw%d" % l, n * b, n * b + n), V("ll%d" % l, 16 * odd + 8, 16 * odd + 8 + k)), ACT.Copy)
+
+    def pairs(l, odd, tile, first, step, op):
+        n, k = C >> l, (7, 4)[l]
+        for b in range(4):
+            tt(V(tile, first + b, 16 * k * step, step),
+               (V("dw%d" % l, n * b, n * b + n), V("ll%d" % l, 16 * odd, 16 * odd + k)),
+               V("g%d" % l, 16 * k * (4 * odd + b), 16 * k * (4 * odd + b + 1)), op)
+
+    def layer(src, a, m, tile, first, step, split):
+        order = (2, 0, 3, 1) if split else range(4)
+        for b in order:
+            mm(4 + b, "qw", 128 * b, src, a, 128)
+        for b in order:
+            out = V(tile, first + b, step * m, step)
+            if split and b >= 2:
+                ts(out, ps(4 + b, 0, m), 0.03125, ALU.mult)
+            else:
+                act(out, ps(4 + b, 0, m), ACT.Copy, scale=0.03125)
+
+    def unpack(bank, src, a, n):
+        for b in range(4):
+            mm(bank + b, "qe", 128 * b, src, a, n)
+
+    def order_rows(l):
+        n = C >> l
+        act(V("olf", C * l, C * l + n), (V("o%d" % l), V("olo", 0, n // 16)), ACT.Identity, bias=float(n // 2))
+
+    orders(0, "qx", "pa_")
+    lists(0, ((3, 4), (2, 3)))
+    fetch(0, 1)
+    pairs(0, 1, "lot", 0, 4, ALU.add)
+    quant("s0", 0, "lot", 0, 128)
+    swap_wide("s0", "r0", "h0")
+    const(V("rz1", 0, None, 5))
+    const(V("rz1", 1041, None, 5))
+    for s in range(2, 5):
+        const(V("rz1", s, None, 5), 1)
+    const(V("ret", 256, 512))
+    const(V("rot", 256, 512))
+    lists(0, ((0, 2),))
+    ts(V("olo"), V("ci", 24, 52), P16, ALU.add, G64, ALU.add)
+    fetch(0, 0)
+    order_rows(0)
+    pairs(0, 1, "ht0", 4, 8, ALU.subtract)
+    pairs(0, 0, "let", 0, 4, ALU.add)
+    quant("mid0", 112, "let", 0, 128)
+    layer("mid0", 112, 104, "at1", 0, 8, False)
+    pairs(0, 0, "ht0", 0, 8, ALU.subtract)
+    quant("qh0", 0, "ht0", 0, 224)
+    scorer("qb", "ubt", "pb_")
+    ts(V("rz1", 1, 1040, 5), V("i32f", 0, 208), PM32, ALU.is_gt)
+    unpack(0, "qh0", 0, 208)
+    for b in range(4):
+        act(V("hw0", C * b, C * b + 208), ps(b, 0, 208), ACT.Copy)
+        if b < 2:
+            act(V("hw0", C * b + 208, C * b + C), ps(b, 0, 208), ACT.Copy, scale=-1.0)
+    quant("s1", 80, "et", 0, 128)
+    quant("s2", 80, "et", 0, 128)
+    quant("qv", 0, "vt", 0, 128)
+    ts(V("la", 32, 58), V("rw0", 0, 26), 1, ALU.bitwise_and)
+    ts(V("la", 0, 26), V("rw0", 0, 26), 1, ALU.arith_shift_right)
+    ts(V("la", 64, 90), V("la", 32, 58), 208.0, ALU.mult)
+    tcopy(V("ua0", 0, 26), V("la", 0, 26))
+    tt(V("la", 96, 122), V("la", 64, 90), V("la", 0, 26), ALU.add)
+    tcopy(V("uh0", 0, 26), V("la", 96, 122))
+    layer("mid0", 8, 104, "at1", 4, 8, True)
+    quant("qa1", 0, "at1", 0, 224)
+
+    orders(1, "qa1", "pb_")
+    lists(1, ((3, 4), (2, 3)))
+    fetch(1, 1)
+    pairs(1, 1, "lot", 0, 4, ALU.add)
+    quant("s1", 0, "lot", 0, 128)
+    swap_narrow("s1", "r1", "h1")
+    send([(hd, V("rl", 0, 13), V("rw1", 0, 13), "hl", eng[q4:2 * q4])])
+    lists(1, ((0, 2),))
+    fetch(1, 0)
+    pairs(1, 1, "ht1", 4, 8, ALU.subtract)
+    pairs(1, 0, "let", 0, 4, ALU.add)
+    quant("mid1", 64, "let", 0, 128)
+    layer("mid1", 64, 64, "ret", 0, 4, False)
+    pairs(1, 0, "ht1", 0, 8, ALU.subtract)
+    quant("qh1", 112, "ht1", 0, 128)
+    send2(hd, hc, "qh1", 112, "rh", 104, "hh")
+    quant("up1", 160, "ret", 0, 128)
+    send2(hc, hd, "up1", 160, "re_", 52, "he")
+
+    def highs(a, odd, even):
+        unpack(0, "qh1", a, 128)
+        for b in range(4):
+            act(V("hm", 208 * b + odd, 208 * b + odd + 52), V("ps%d" % b, 1, 104, 2), ACT.Copy)
+            act(V("hm", 208 * b + even, 208 * b + even + 52), V("ps%d" % b, 0, 104, 2), ACT.Copy)
+
+    def plus_minus(ab, w, a, m, bank, hw, h):
+        tt(V(ab, w + a, w + a + m), ps(bank, 0, m), V(hw, h + a, h + a + m), ALU.add)
+        tt(V(ab, w + 208 + a, w + 208 + a + m), ps(bank, 0, m), V(hw, h + a, h + a + m), ALU.subtract)
+
+    highs(112, 0, 156)
+    layer("mid1", 12, 64, "rot", 0, 4, True)
+    quant("s2", 0, "rot", 0, 128)
+    swap_narrow("s2", "r2", "h2")
+    send([(p3, V("up1c", 56, 108), V("s2c", 0, 52), "a3", off[:len(off) // 2])])
+    send([(p3, V("up1s", 56, 108), V("s2s", 0, 52), "a3", off[len(off) // 2:])])
+
+    tcopy(V("hs0", 0, C), (V("hw0", 0, C), V("uh0", 0, 26)))
+    act(V("hs0", C, 2 * C), (V("hw0", C, 2 * C), V("uh0", 0, 26)), ACT.Copy)
+    order_rows(1)
+    dma("S", T.ol[:], T.olf[0:128:16, :], [V("olf")], [])
+    highs(8, 52, 104)
+    ts(V("lb", 0, 13), V("rw1", 0, 13), EVENP, ALU.mult)
+    ts(V("lb", 16, 29), V("lst", 0, 13), ODDP, ALU.mult)
+    both = V("lb", 32, 45)
+    tt(both, V("lb", 0, 13), V("lb", 16, 29), ALU.add)
+    ts(V("lb", 64, 77), both, 1, ALU.bitwise_and)
+    ts(V("lb", 80, 93), both, 2, ALU.arith_shift_right)
+    ts(V("lb", 96, 109), both, 1, ALU.arith_shift_right, 1, ALU.bitwise_and)
+    ts(V("lb", 112, 125), V("lb", 64, 77), 208.0, ALU.mult, CA1, ALU.add)
+    ts(V("lb", 128, 141), V("lb", 96, 109), CA2, ALU.mult)
+    tt(V("lb", 48, 61), V("lb", 112, 125), V("lb", 80, 93), ALU.add)
+    tt(V("lb", 144, 157), V("lb", 128, 141), V("lb", 48, 61), ALU.add)
+    tcopy(V("uh1", 0, 13), V("lb", 144, 157))
+    unpack(4, "up1", 108, 128)
+    for b in range(4):
+        plus_minus("ab1", C * b, 104, 104, 4 + b, "hm", 208 * b)
+    unpack(0, "up1", 4, 128)
+    for b in range(4):
+        plus_minus("ab1", C * b, 0, 104, b, "hm", 208 * b)
+        out, src = V("u1t", b, None, 4), (V("ab1", C * b, C * b + C), V("uh1", 0, 13))
+        if b < 3:
+            act(out, src, ACT.Copy)
+        else:
+            tcopy(out, src)
+    quant("qu1", 0, "u1t", 0, 208)
+
+    for b in (2, 0, 3, 1):
+        mm(4 + b, "qe", 128 * b, "qu1", 0, 208)
+    for b in range(2):
+        plus_minus("ab0", C * b, 0, 208, 6 + b, "hw0", C * (2 + b))
+        act(V("da0", 208 * b, 208 * b + 208), ps(4 + b, 0, 208), ACT.Copy)
+    parts = ((0, 288), (288, C))
+    for a, e in parts:
+        for b in range(2):
+            act(V("u0t", 4 * a + 2 + b, 4 * e, 4), (V("ab0", C * b, C * b + C), V("uh0", a // 16, e // 16)), ACT.Copy)
+    for h, (a, e) in enumerate(parts):
+        for b in range(2):
+            tt(V("u0t", 4 * a + b, 4 * e, 4), (V("da0", 208 * b, 208 * b + 208), V("ua0", a // 16, e // 16)),
+               V("hs0", C * b + a, C * b + e), ALU.add)
+        quant("qu0", a, "u0t", a, e - a)
+        mm(h, "qv", 0, "qu0", a, e - a)
+        dma("S", T.oc[:, 4 * a:4 * e], T.qu0c[:, a:e].bitcast(dt.uint8), [V("qu0c", a, e)], [])
+        for k in range(4):
+            dma("S", T.osc[4 * k:4 * k + 4, a:e], T.qu0s[32 * k:32 * k + 4, a:e], [V("qu0s", a, e)], [])
+        act(V("yt", a, e), ps(h, 0, e - a), ACT.Copy)
+        dma("A", T.y[:, a:e], T.yt[:, a:e], [V("yt", a, e)], [])
+
+    for sem, n in count.items():
+        if clock["G"].get(sem, 0) < n:
+            g.wait_ge(T.sem[sem], n)

@@ -6,8 +6,7 @@ ALU = AluOpType
 ACT = ActivationFunctionType
 C = 416
 BIG = 2.0e29
-ON_VECTOR = ((4, 5), (1, 2))
-ROWS = (2, 2)
+ON_VECTOR = ((5, 5), (2, 2))
 CUTS = ((0, 5, 8, 10, 13), (0, 3, 5, 7))
 X4, U8, BF, F32, I32, U16 = "float8_e4m3fn_x4", "uint8", "bfloat16", "float32", "int32", "uint16"
 
@@ -25,14 +24,14 @@ def _mx(name, n):
 
 for _n, _w in (("xt", 4 * C), ("uat", 512), ("ubt", 512), ("vt", 512), ("et", 2048), ("ones", 128),
                ("ident", 128), ("jv", C), ("rz0", 8 * 160), ("rz1", 5 * 224), ("z0", 2 * 8 * C), ("z1", 2 * 5 * 224),
-               ("zs", 2 * 8 * C), ("sg", 4800), ("jk", 14 * 96), ("tt", 2 * C), ("o0", 896), ("o1", 512), ("to", 1024),
+               ("zs", 2 * 8 * C), ("sg", 3840), ("jk", 14 * 96), ("tt", 2 * C), ("o0", 896), ("o1", 512), ("to", 1024),
                ("dw0", 4 * C), ("dw1", 4 * 208), ("g0", 8 * 112), ("g1", 8 * 64), ("lot", 512), ("let", 512),
                ("ht0", 4 * 224), ("ht1", 512), ("at1", 4 * 224), ("ret", 512), ("rot", 512), ("hw0", 4 * C),
                ("hm", 4 * 208), ("hs0", 2 * C), ("ab1", 4 * C), ("ab0", 2 * C), ("da0", 2 * 208), ("u1t", 4 * 208),
                ("u0t", 4 * C)):
     _buf(_n, _w, BF)
 for _n, _w in (("i32f", 224), ("tm", 2 * C), ("cum", 1056), ("rsa", 32), ("rsb0", 32), ("rsb1", 32), ("rsc", 96),
-               ("rk", 32), ("xp", 64), ("wt", 96), ("wl", 32), ("cf", 16), ("olf", C + C // 2), ("yt", C)):
+               ("rk", 1024), ("xp", 64), ("wt", 96), ("wl", 32), ("cf", 16), ("olf", C + C // 2), ("yt", C)):
     _buf(_n, _w, F32)
 for _n, _w in (("ci", 52), ("rw0", 28), ("rw1", 16), ("pa", 64), ("la", 160), ("lb", 160), ("lst", 16), ("rl", 16)):
     _buf(_n, _w, I32)
@@ -378,24 +377,23 @@ def rank_program(g, core, T, topo):
 
     for b in range(4):
         act(V("et", 512 * b + b, 512 * b + 512, 4), V("ident"), ACT.Copy)
-    quant("qe", 0, "et", 0, 512)
     ts(V("rz0", 1, None, 8), V("i32f", 0, 160), PM32, ALU.is_gt)
     for s in range(2, 5):
         act(V("rz0", s, None, 8), V("et", 0, 160), ACT.Identity, bias=1.0, scale=0.0)
+    quant("s0", 80, "et", 0, 128)
+    quant("qe", 0, "et", 0, 256)
     scorer("qa", "uat", "pa_")
     for s in range(5, 8):
         act(V("rz0", s, None, 8), V("et", 0, 160), ACT.Identity, bias=1.0, scale=0.0)
     act(EVENG, ODDG, ACT.Identity, bias=1.0, scale=-1.0)
     act(G64, ODDG, ACT.Copy, scale=64.0)
-    act(GBIG, ODDG, ACT.Copy, scale=BIG)
-    act(EVENP, ODDP, ACT.Identity, bias=1.0, scale=-1.0)
-    act(CA1, ODDP, ACT.Identity, bias=156.0, scale=-52.0)
-    act(CA2, ODDP, ACT.Identity, bias=-156.0, scale=104.0)
+    act(col("cf", 12), PM32, ACT.Identity, bias=192.0)
     const(V("rsa"))
     const(V("rsb0"))
     const(V("z0", 1, None, 8))
     const(V("rz0", 0, None, 8))
     iota(V("jv"), [[1, C]], -(C // 2))
+    const(V("rk", 992, 1024))
     const(V("o0"))
     const(V("to", 0, None, 16))
     const(V("lot", 448, 512))
@@ -417,7 +415,7 @@ def rank_program(g, core, T, topo):
     dma("S", T.qwc[:].bitcast(dt.uint8), T.wc[:], [], [V("qwc")])
     dma("S", T.qws[:], T.ws[:], [], [V("qws")])
     dma("S", T.vt[:], T.v[:], [], [V("vt")])
-    quant("s0", 80, "et", 0, 128)
+    quant("qe", 256, "et", 256, 256)
 
     def orders(l, state_, scorer_):
         on_vector, cuts = ON_VECTOR[l], CUTS[l]
@@ -441,17 +439,18 @@ def rank_program(g, core, T, topo):
             return col("tm", e * w + 32 * b) if 32 * b + 32 <= n else col("cf", 10 + e)
 
         def diagonal(e):
+            tt(zv(e, 0, 0, w), ps(e, 0, w), V("tm", e * w, e * w + w), ALU.is_gt)
+
+        def short(e):
             if n < w:
                 ts(scal(e, nb - 1), col("tm", e * w + w - 32), GBIG, ALU.add)
-            tt(zv(e, 0, 0, w), ps(e, 0, w), V("tm", e * w, e * w + w), ALU.is_gt)
 
         turn(V("tm", 32 * mid, w), ps(0, 32 * mid, w))
         turn(V("tm", 0, 32 * mid), ps(0, 0, 32 * mid))
-        if n < w:
-            diagonal(0)
+        short(0)
         turn(V("tm", w, 2 * w), ps(1, 0, w))
-        if n == w:
-            diagonal(0)
+        diagonal(0)
+        short(1)
         diagonal(1)
         pcs = pieces(nb, dd)
         later, at = [], [0]
@@ -462,32 +461,26 @@ def rank_program(g, core, T, topo):
                 sg = V("sg", at[0], at[0] + k1 - k0)
                 at[0] += k1 - k0
                 act(sg, ps(2 + e, k0, k1), ACT.Sign, bias=scal(e, b), scale=-1.0)
-                if later:
-                    act(*later.pop())
+                if len(later) > l:
+                    act(*later.pop(0))
                 acc = col(rsb if second else "rsa", 16 * e + b)
                 if wrapped:
                     later.append((zv(e, s, k0, k1), sg, ACT.Sign, 1.0, -1.0, acc))
                 else:
                     later.append((zv(e, s, k0, k1), sg, ACT.Relu, None, -1.0, acc))
-        act(*later.pop())
+        while later:
+            act(*later.pop(0))
+        for b in range(4):
+            act(V(dw, n * b, n * b + n), ps(4 + b, 0, n), ACT.Copy, scale=0.5)
         hl = 16 * dd
         for e in range(2):
             for b, lo, hi, wrapped, second, s in pcs[:on_vector[e]]:
                 ts(zv(e, s, 32 * lo, 32 * hi), ps(e, 32 * lo, 32 * hi), scal(e, b), ALU.is_gt)
-        keep = (on_vector[0], on_vector[1] - ROWS[l])
-        for b, lo, hi, wrapped, second, s in pcs[keep[1]:on_vector[1]]:
-            act(V("sg", at[0], at[0] + 2 * hl), zv(1, s, 32 * lo, 32 * hi), ACT.Identity, accum=col("rsa", 16 + b))
-            at[0] += 2 * hl
-        for b in range(4):
-            act(V(dw, n * b, n * b + n), ps(4 + b, 0, n), ACT.Copy, scale=0.5)
         for e in range(2):
-            for b, lo, hi, wrapped, second, s in pcs[:keep[e]]:
+            for b, lo, hi, wrapped, second, s in pcs[:on_vector[e]]:
                 j = (7 * e + b) * hl
                 scan(V("jk", j, j + hl), zv(e, s, 32 * lo, 32 * lo + hl), zv(e, s, 32 * lo + hl, 32 * hi), ALU.add,
                      ALU.add)
-        for e in range(2):
-            if keep[e]:
-                tcopy(V("rsa", 16 * e, 16 * e + keep[e]), V("jk", 7 * e * hl + hl - 1, (7 * e + keep[e]) * hl, hl))
 
         def columns(e, u0, u1):
             a, b = (e * w + 32 * u0) * S, (e * w + 32 * u1) * S
@@ -498,33 +491,41 @@ def rank_program(g, core, T, topo):
             a, b = e * w + 32 * u0, e * w + 32 * u1
             turn(V("tt", a, b), V("zs", a * S + S - 1, b * S, S))
 
-        def fold(e, u0, u1):
-            a, b, c = e * w + 32 * u0, e * w + 32 * u1, 512 * e + 32 + 32 * u0
-            scan(V("cum", c, c + b - a), V("zs", a * S + 1, b * S, S), V("tt", a, b), ALU.add, ALU.subtract,
-                 col("cum", c - 1) if u0 else 0.0)
+        def fold(e, u0, u1, out, first):
+            a, b = e * w + 32 * u0, e * w + 32 * u1
+            scan(out, V("zs", a * S + 1, b * S, S), V("tt", a, b), ALU.add, ALU.subtract, first)
 
+        last = cuts[-2]
         for i in range(len(cuts) - 1):
             columns(0, cuts[i], cuts[i + 1])
-        flip(0, 0, nb)
+            if i == 0:
+                for e in range(2):
+                    tcopy(V("rsa", 16 * e, 16 * e + on_vector[e]),
+                          V("jk", 7 * e * hl + hl - 1, (7 * e + on_vector[e]) * hl, hl))
         columns(1, cuts[0], cuts[1])
-        fold(0, 0, nb)
+        flip(0, 0, nb)
         for i in range(1, len(cuts) - 2):
             columns(1, cuts[i], cuts[i + 1])
-        last = cuts[-2]
+        fold(0, 0, nb, V("cum", 32, 32 + w), 0.0)
         flip(1, 0, last)
         columns(1, last, nb)
-        fold(1, 0, last)
+        fold(1, 0, last, V("cum", 544, 544 + 32 * last), 0.0)
+        m, rk, base = 16 + last, 992, col("cf", 12 + l)
+        tt(V("rsc", 0, m), V("rsa", 0, m), V(rsb, 0, m), ALU.add)
         flip(1, last, nb)
-        tt(V("rsc", 0, 32), V("rsa"), V(rsb), ALU.add)
-        fold(1, last, nb)
-        ts(V("rsc", 32, 64), V("rsc", 0, 32), PM32, ALU.add, float(32 * dd), ALU.add)
-        tt(V("rsc", 64, 96), V("cum", 63, 1056, 32), V("cum", 31, 1024, 32), ALU.subtract)
-        tt(V("rk"), V("rsc", 64, 96), V("rsc", 32, 64), ALU.add)
+        for b in range(last, nb):
+            ts(col("rsc", 16 + b), col("rsa", 16 + b), col(rsb, 16 + b), ALU.add, base, ALU.add)
+        tt(V("rsc", 64, 64 + m), V("cum", 63, 63 + 32 * m, 32), V("cum", 31, 31 + 32 * m, 32), ALU.subtract)
+        ts(V("rsc", 32, 32 + m), V("rsc", 0, m), base, ALU.add)
+        for b in range(last, nb):
+            fold(1, b, b + 1, V("rk", 16 + b, 1024, 32), col("rsc", 16 + b))
+            if b == last:
+                tt(V("rk", rk, rk + m), V("rsc", 64, 64 + m), V("rsc", 32, 32 + m), ALU.add)
         rw, o = "rw%d" % l, "o%d" % l
-        turn(V("xp", 16, 48), V("rk"))
-        ts(V("wt", 64, 80), V("rk", 0, 16), EVENG, ALU.mult)
+        ts(V("wt", 64, 80), V("rk", rk, rk + 16), EVENG, ALU.mult)
+        turn(V("xp", 16, 48), V("rk", rk, rk + 32))
+        ts(V("wt", 80, 96), V("rk", rk + 16, rk + 32), ODDG, ALU.mult)
         turn(V("wt", 0, 64), V("xp"))
-        ts(V("wt", 80, 96), V("rk", 16, 32), ODDG, ALU.mult)
         tt(V(rw, 0, 2 * nb, 2), V("wt", 64, 64 + nb), V("wt", 16, 16 + nb), ALU.add)
         tt(V(rw, 1, 2 * nb, 2), V("wt", 80, 80 + nb), V("wt", 32, 32 + nb), ALU.add)
         t = n // 16
@@ -540,8 +541,10 @@ def rank_program(g, core, T, topo):
         for s0, s1 in runs:
             for s in range(s0, s1):
                 turn(V("to", 256 * s, 256 * s + wo // 4), V(o, s, wo, 4))
+        for s0, s1 in runs:
             a, b = 256 * s0, 256 * s1
             tt(V("wl", 8 * s0, 8 * s1), V("to", a, b, 32), V("to", a + 16, b, 32), ALU.add)
+        for s0, s1 in runs:
             ts(V("ll%d" % l, 8 * s0, 8 * s1), V("wl", 8 * s0, 8 * s1), float(n // 2), ALU.add)
 
     def fetch(l, odd):
@@ -577,6 +580,11 @@ def rank_program(g, core, T, topo):
         act(V("olf", C * l, C * l + n), (V("o%d" % l), V("olo", 0, n // 16)), ACT.Identity, bias=float(n // 2))
 
     orders(0, "qx", "pa_")
+    act(GBIG, ODDG, ACT.Copy, scale=BIG)
+    act(EVENP, ODDP, ACT.Identity, bias=1.0, scale=-1.0)
+    act(CA1, ODDP, ACT.Identity, bias=156.0, scale=-52.0)
+    act(CA2, ODDP, ACT.Identity, bias=-156.0, scale=104.0)
+    act(col("cf", 13), PM32, ACT.Identity, bias=96.0)
     lists(0, ((3, 4), (2, 3)))
     fetch(0, 1)
     pairs(0, 1, "lot", 0, 4, ALU.add)
@@ -605,25 +613,25 @@ def rank_program(g, core, T, topo):
         act(V("hw0", C * b, C * b + 208), ps(b, 0, 208), ACT.Copy)
         if b < 2:
             act(V("hw0", C * b + 208, C * b + C), ps(b, 0, 208), ACT.Copy, scale=-1.0)
-    quant("s1", 80, "et", 0, 128)
-    quant("s2", 80, "et", 0, 128)
-    quant("qv", 0, "vt", 0, 128)
     ts(V("la", 32, 58), V("rw0", 0, 26), 1, ALU.bitwise_and)
     ts(V("la", 0, 26), V("rw0", 0, 26), 1, ALU.arith_shift_right)
+    quant("s1", 80, "et", 0, 128)
     ts(V("la", 64, 90), V("la", 32, 58), 208.0, ALU.mult)
     tcopy(V("ua0", 0, 26), V("la", 0, 26))
+    quant("s2", 80, "et", 0, 128)
     tt(V("la", 96, 122), V("la", 64, 90), V("la", 0, 26), ALU.add)
+    quant("qv", 0, "vt", 0, 128)
     tcopy(V("uh0", 0, 26), V("la", 96, 122))
     layer("mid0", 8, 104, "at1", 4, 8, True)
     quant("qa1", 0, "at1", 0, 224)
 
     orders(1, "qa1", "pb_")
+    send([(hd, V("rl", 0, 13), V("rw1", 0, 13), "hl", eng[:q4])])
     lists(1, ((3, 4), (2, 3)))
     fetch(1, 1)
     pairs(1, 1, "lot", 0, 4, ALU.add)
     quant("s1", 0, "lot", 0, 128)
     swap_narrow("s1", "r1", "h1")
-    send([(hd, V("rl", 0, 13), V("rw1", 0, 13), "hl", eng[q4:2 * q4])])
     lists(1, ((0, 2),))
     fetch(1, 0)
     pairs(1, 1, "ht1", 4, 8, ALU.subtract)
@@ -647,24 +655,24 @@ def rank_program(g, core, T, topo):
         tt(V(ab, w + 208 + a, w + 208 + a + m), ps(bank, 0, m), V(hw, h + a, h + a + m), ALU.subtract)
 
     highs(112, 0, 156)
+    ts(V("lb", 0, 13), V("rw1", 0, 13), EVENP, ALU.mult)
+    ts(V("lb", 16, 29), V("lst", 0, 13), ODDP, ALU.mult)
+    both = V("lb", 32, 45)
+    tt(both, V("lb", 0, 13), V("lb", 16, 29), ALU.add)
     layer("mid1", 12, 64, "rot", 0, 4, True)
     quant("s2", 0, "rot", 0, 128)
     swap_narrow("s2", "r2", "h2")
     send([(p3, V("up1c", 56, 108), V("s2c", 0, 52), "a3", off[:len(off) // 2])])
     send([(p3, V("up1s", 56, 108), V("s2s", 0, 52), "a3", off[len(off) // 2:])])
 
+    ts(V("lb", 64, 77), both, 1, ALU.bitwise_and)
+    ts(V("lb", 80, 93), both, 2, ALU.arith_shift_right)
+    ts(V("lb", 96, 109), both, 1, ALU.arith_shift_right, 1, ALU.bitwise_and)
     tcopy(V("hs0", 0, C), (V("hw0", 0, C), V("uh0", 0, 26)))
     act(V("hs0", C, 2 * C), (V("hw0", C, 2 * C), V("uh0", 0, 26)), ACT.Copy)
     order_rows(1)
     dma("S", T.ol[:], T.olf[0:128:16, :], [V("olf")], [])
     highs(8, 52, 104)
-    ts(V("lb", 0, 13), V("rw1", 0, 13), EVENP, ALU.mult)
-    ts(V("lb", 16, 29), V("lst", 0, 13), ODDP, ALU.mult)
-    both = V("lb", 32, 45)
-    tt(both, V("lb", 0, 13), V("lb", 16, 29), ALU.add)
-    ts(V("lb", 64, 77), both, 1, ALU.bitwise_and)
-    ts(V("lb", 80, 93), both, 2, ALU.arith_shift_right)
-    ts(V("lb", 96, 109), both, 1, ALU.arith_shift_right, 1, ALU.bitwise_and)
     ts(V("lb", 112, 125), V("lb", 64, 77), 208.0, ALU.mult, CA1, ALU.add)
     ts(V("lb", 128, 141), V("lb", 96, 109), CA2, ALU.mult)
     tt(V("lb", 48, 61), V("lb", 112, 125), V("lb", 80, 93), ALU.add)
@@ -674,8 +682,9 @@ def rank_program(g, core, T, topo):
     for b in range(4):
         plus_minus("ab1", C * b, 104, 104, 4 + b, "hm", 208 * b)
     unpack(0, "up1", 4, 128)
-    for b in range(4):
+    for b in (0, 3, 1, 2):
         plus_minus("ab1", C * b, 0, 104, b, "hm", 208 * b)
+    for b in range(4):
         out, src = V("u1t", b, None, 4), (V("ab1", C * b, C * b + C), V("uh1", 0, 13))
         if b < 3:
             act(out, src, ACT.Copy)
@@ -699,10 +708,11 @@ def rank_program(g, core, T, topo):
         quant("qu0", a, "u0t", a, e - a)
         mm(h, "qv", 0, "qu0", a, e - a)
         dma("S", T.oc[:, 4 * a:4 * e], T.qu0c[:, a:e].bitcast(dt.uint8), [V("qu0c", a, e)], [])
-        for k in range(4):
-            dma("S", T.osc[4 * k:4 * k + 4, a:e], T.qu0s[32 * k:32 * k + 4, a:e], [V("qu0s", a, e)], [])
+        if h == 1:
+            for k in range(4):
+                dma("S" if k < 2 else "A", T.osc[4 * k:4 * k + 4, :], T.qu0s[32 * k:32 * k + 4, :], [V("qu0s")], [])
         act(V("yt", a, e), ps(h, 0, e - a), ACT.Copy)
-        dma("A", T.y[:, a:e], T.yt[:, a:e], [V("yt", a, e)], [])
+        dma("A" if h == 0 else "S", T.y[:, a:e], T.yt[:, a:e], [V("yt", a, e)], [])
 
     for sem, n in count.items():
         if clock["G"].get(sem, 0) < n:

@@ -5,10 +5,24 @@ from concourse.mybir import dt, AluOpType, ActivationFunctionType
 ALU = AluOpType
 ACT = ActivationFunctionType
 C = 416
-BIG = 2.0e29
-ON_VECTOR = ((5, 5), (2, 2))
-CUTS = ((0, 5, 8, 10, 13), (0, 3, 5, 7))
+BIG = 2.0 ** 96
+STEP, DROP, LOW = 512.0, 16384.0, 1024.0
+ON_SCALAR = (9, 3)
+QUANT_AT = ({0: 6, 1: 13}, {0: 5})
+FIRST = (32, 32)
+JW = 128
 X4, U8, BF, F32, I32, U16 = "float8_e4m3fn_x4", "uint8", "bfloat16", "float32", "int32", "uint16"
+
+
+def planes(nb):
+    lens = [16 * (nb - i) for i in range(nb)]
+    out, at = [], 0
+    for k in range(0, nb, 4):
+        w = max(128, lens[k])
+        out.append((at, w, lens[k + 3] if k + 3 < nb else 0))
+        at += w
+    return out, at
+
 
 SCRATCH = {}
 
@@ -22,26 +36,27 @@ def _mx(name, n):
     _buf(name + "s", n, U8)
 
 
-for _n, _w in (("xt", 4 * C), ("uat", 512), ("ubt", 512), ("vt", 512), ("et", 2048), ("ones", 128),
-               ("ident", 128), ("jv", C), ("rz0", 8 * 160), ("rz1", 5 * 224), ("z0", 2 * 8 * C), ("z1", 2 * 5 * 224),
-               ("zs", 2 * 8 * C), ("sg", 3840), ("jk", 14 * 96), ("tt", 2 * C), ("o0", 896), ("o1", 512), ("to", 1024),
-               ("dw0", 4 * C), ("dw1", 4 * 208), ("g0", 8 * 112), ("g1", 8 * 64), ("lot", 512), ("let", 512),
-               ("ht0", 4 * 224), ("ht1", 512), ("at1", 4 * 224), ("ret", 512), ("rot", 512), ("hw0", 4 * C),
-               ("hm", 4 * 208), ("hs0", 2 * C), ("ab1", 4 * C), ("ab0", 2 * C), ("da0", 2 * 208), ("u1t", 4 * 208),
-               ("u0t", 4 * C)):
+for _n, _w in (("xt", 4 * C), ("uat", 512), ("ubt", 512), ("vt", 512), ("et", 2048), ("gst", 512),
+               ("ident", 128), ("eq", 432), ("km", C), ("k1", C), ("kr", C),
+               ("k4", C), ("k32", C), ("z0", 4 * planes(26)[1]), ("z1", 4 * planes(13)[1]), ("sg", 2 * C),
+               ("jk", 26 * JW), ("rd", C), ("dw0", 4 * C), ("dw1", 4 * 208), ("g0", 2 * C), ("g1", C), ("lot", 512),
+               ("let", 512), ("ht0", 4 * 208), ("ht1", 1024), ("at1", 4 * 208), ("ret", 512), ("rot", 512),
+               ("hw0", 4 * C), ("hm", 4 * 156), ("hs0", 4 * C), ("abe", 512), ("abl", 2 * C),
+               ("dq", 4 * C), ("xb", C), ("tb", C), ("u0t", 4 * C)):
     _buf(_n, _w, BF)
-for _n, _w in (("i32f", 224), ("tm", 2 * C), ("cum", 1056), ("rsa", 32), ("rsb0", 32), ("rsb1", 32), ("rsc", 96),
-               ("rk", 1024), ("xp", 64), ("wt", 96), ("wl", 32), ("cf", 16), ("olf", C + C // 2), ("yt", C)):
+for _n, _w in (("kc", C), ("dm", C), ("own", C), ("xo", C), ("rs", 32), ("rr", 32), ("cnt", 32), ("cf", 24), ("jv", C),
+               ("o0", C), ("o1", 224), ("xl", C), ("yt", C)):
     _buf(_n, _w, F32)
-for _n, _w in (("ci", 52), ("rw0", 28), ("rw1", 16), ("pa", 64), ("la", 160), ("lb", 160), ("lst", 16), ("rl", 16)):
+for _n, _w in (("ci", 24), ("rw0", 28), ("rw1", 16), ("la", 128), ("lb", 128), ("lst", 16), ("rl", 16)):
     _buf(_n, _w, I32)
-for _n, _w in (("uof", 16), ("pos", 28), ("ll0", 32), ("ll1", 32), ("olo", 28), ("ua0", 28), ("uh0", 28), ("uh1", 14)):
+for _n, _w in (("uof", 8), ("pos0", 26), ("pos1", 14), ("ll0", 104), ("ll1", 56), ("kk", 26), ("lq", 104)):
     _buf(_n, _w, U16)
-for _n, _w in (("qx", C), ("qa", 128), ("qb", 128), ("qv", 128), ("pa_", 256), ("pb_", 256), ("qe", 512), ("qw", 512),
-               ("s0", 208), ("s1", 208), ("s2", 208), ("mid0", 240), ("mid1", 192), ("qa1", 224), ("qh0", 224),
-               ("qh1", 240), ("up1", 288), ("qu1", 208), ("qu0", C)):
+for _n, _w in (("qx", C), ("qa", 128), ("qb", 128), ("qv", 128), ("pa_", 128), ("pb_", 128), ("qe", 512), ("qw", 512),
+               ("qg", 128), ("qz0", planes(26)[1]), ("qz1", planes(13)[1]), ("s0", 208), ("s1", 208), ("s2", 208),
+               ("mid0", 240), ("mid1", 192), ("qa1", 208), ("qh0", 208), ("qh1", 320), ("up1", 240), ("qab", 448),
+               ("qu0", C)):
     _mx(_n, _w)
-for _n, _w, _v in (("r0", 52, 208), ("r1", 52, 208), ("r2", 52, 208), ("rh", 104, 104), ("re_", 52, 52)):
+for _n, _w, _v in (("r0", 52, 208), ("r1", 52, 208), ("r2", 52, 208), ("rh", 52, 52), ("re_", 104, 104)):
     _buf(_n + "c", _w, X4)
     _buf(_n + "s", _v, U8)
 for _k in range(8):
@@ -66,25 +81,6 @@ def helpers(core, far, topo):
     return near[0], near[1], other[0], other[1]
 
 
-def pieces(nb, dd):
-    out = []
-    for b in range(nb):
-        lo, hi = b + 1, b + dd + 1
-        if hi <= nb:
-            out.append([b, lo, hi, False, 0])
-        elif lo >= nb:
-            out.append([b, 0, hi - nb, True, 0])
-        else:
-            out.append([b, lo, nb, False, 0])
-            out.append([b, 0, hi - nb, True, 1])
-    ends = [0] * dd
-    for p in sorted(out, key=lambda p: p[1]):
-        s = ends.index(p[1])
-        ends[s] = p[2]
-        p.append(s + 2)
-    return out
-
-
 def relay_program(g, core, T, topo, r):
     me = T.cores[r]
     p1, p2 = T.cores[r ^ 1], T.cores[r ^ 2]
@@ -107,28 +103,28 @@ def relay_program(g, core, T, topo, r):
         g.wait_ge(T.sem.h1, 2 * quarter)
         on(p2, cod("mid1c", 12, 64), cod("r1c", 0, 52), "a1")
         g.wait_ge(T.sem.h2, 2 * quarter)
-        on(p2, cod("up1c", 4, 56), cod("r2c", 0, 52), "a2")
+        on(p2, cod("up1c", 8, 60), cod("r2c", 0, 52), "a2")
     elif core == hb:
         g.wait_ge(T.sem.h0, quarter)
         on(p1, T.mid0s[:, 8:112], T.r0s[:, 0:104], "a0")
         g.wait_ge(T.sem.h1, 2 * quarter)
         on(p2, T.mid1s[:, 12:64], T.r1s[:, 0:52], "a1")
         g.wait_ge(T.sem.h2, 2 * quarter)
-        on(p2, T.up1s[:, 4:56], T.r2s[:, 0:52], "a2")
+        on(p2, T.up1s[:, 8:60], T.r2s[:, 0:52], "a2")
     elif core == hc:
         g.wait_ge(T.sem.h0, quarter)
         on(p1, cod("mid0c", 60, 112), cod("r0c", 0, 52), "a0")
         g.wait_ge(T.sem.hh, 2 * quarter)
-        on(p1, T.qh1s[:, 8:112], T.rhs[:, 0:104], "ah")
+        on(p1, T.qh1s[:, 12:64], T.rhs[:, 0:52], "ah")
         g.wait_ge(T.sem.he, 2 * quarter)
-        on(p1, cod("up1c", 108, 160), cod("re_c", 0, 52), "ae")
+        on(p1, cod("qabc", 8, 112), cod("re_c", 0, 104), "ae")
     elif core == hd:
         g.wait_ge(T.sem.hl, quarter)
         on(p1, T.lst[:, 0:13], T.rl[:, 0:13], "al")
         g.wait_ge(T.sem.hh, 2 * quarter)
-        on(p1, cod("qh1c", 8, 112), cod("rhc", 0, 104), "ah")
+        on(p1, cod("qh1c", 12, 64), cod("rhc", 0, 52), "ah")
         g.wait_ge(T.sem.he, 2 * quarter)
-        on(p1, T.up1s[:, 108:160], T.re_s[:, 0:52], "ae")
+        on(p1, T.qabs[:, 8:112], T.re_s[:, 0:104], "ae")
     if total[0]:
         g.wait_ge(T.sem.sent, total[0])
 
@@ -201,8 +197,8 @@ def rank_program(g, core, T, topo):
             state(v[0])[0][cols(v)] = tid
         return tid
 
-    def run(q, reads, writes, call):
-        before(q, reads, writes)
+    def run(q, reads, writes, call, adds=False):
+        before(q, reads, [] if adds else writes)
         sem = "c" + q
         count[sem] = count.get(sem, 0) + 1
         call().then_inc(T.sem[sem], 1)
@@ -290,11 +286,12 @@ def rank_program(g, core, T, topo):
         c, s, t = V(name + "c", a, a + n), V(name + "s", a, a + n), V(tile, 4 * t0, 4 * (t0 + n))
         return run("V", [t], [c, s], lambda: g.vector.quantize_mx(ap(c), ap(s), ap(t)))
 
-    def mm(bank, w, w0, x, x0, n):
+    def mm(bank, w, w0, x, x0, n, start=True, stop=True):
         vs = [V(w + "c", w0, w0 + 128), V(w + "s", w0, w0 + 128), V(x + "c", x0, x0 + n), V(x + "s", x0, x0 + n)]
         out = V("ps%d" % bank, 0, n)
         return run("P", vs, [out],
-                   lambda: g.tensor.matmul_mx(ap(out), ap(vs[0]), ap(vs[1]), ap(vs[2]), ap(vs[3]), True, True))
+                   lambda: g.tensor.matmul_mx(ap(out), ap(vs[0]), ap(vs[1]), ap(vs[2]), ap(vs[3]), start, stop),
+                   adds=not start)
 
     def ps(bank, a, b):
         return V("ps%d" % bank, a, b)
@@ -342,31 +339,41 @@ def rank_program(g, core, T, topo):
 
     lands("a0", 3 * nfar, mxv("mid0", 8, 112))
     lands("a1", 2 * nfar, mxv("mid1", 12, 64))
-    lands("a2", 2 * nfar, mxv("up1", 4, 56))
-    lands("a3", len(off), mxv("up1", 56, 108))
-    lands("ae", 2 * nfar, mxv("up1", 108, 160))
-    lands("ah", 2 * nfar, mxv("qh1", 8, 112))
+    lands("a2", 2 * nfar, mxv("up1", 8, 60))
+    lands("a3", len(off), mxv("up1", 60, 112))
+    lands("ae", 2 * nfar, mxv("qab", 8, 112))
+    lands("ah", 2 * nfar, mxv("qh1", 12, 64))
     lands("al", nfar, [V("lst", 0, 13)])
 
     dma("A", T.uat[:], T.ua[:], [], [V("uat")])
     dma("S", T.xt[:, 0:832], T.x[:, 0:832], [], [V("xt", 0, 832)])
     dma("S", T.xt[:, 832:1664], T.x[:, 832:1664], [], [V("xt", 832, 1664)])
+
+    def tails(l, ks):
+        for k in ks:
+            at, w, short = planes(26 >> l)[0][k]
+            const(V("z%d" % l, 4 * (at + short), 4 * (at + w)))
+
     iota(col("ci", 0), [[0, 1]], 0, 1)
-    iota(V("ci", 8, 24), [[16, 2], [32, 4], [0, 2]])
-    const(V("ones"), 1)
-    run("G", [V("ones")], [V("ident")],
-        lambda: g.affine_select(ap(V("ident")), ap(V("ones")), [[-1, 128]], ALU.is_equal, 0.0, 0, 1))
-    iota(V("i32f"), [[0, 7], [1, 32]])
+    iota(V("ident"), [[1, 128]])
+    iota(V("eq"), [[0, 27], [1, 16]])
+    iota(V("ci", 8, 16), [[16, 8]])
+    iota(V("gst"), [[1, 8], [0, 64]])
+    tails(0, (0, 2, 3, 1, 4, 5, 6))
+    const(V("kr"), 1)
+    const(V("kr", 0, None, 16))
     fill(V("et"), 0.0)
-    ts(col("ci", 1), col("ci", 0), 31, ALU.bitwise_and)
-    ts(col("ci", 2), col("ci", 0), 4, ALU.arith_shift_right, 1, ALU.bitwise_and)
+    ts(col("ci", 1), col("ci", 0), 15, ALU.bitwise_and)
+    ts(col("ci", 2), col("ci", 0), 4, ALU.arith_shift_right)
     ts(col("ci", 3), col("ci", 0), 1, ALU.bitwise_and)
-    ts(col("ci", 4), col("ci", 0), 15, ALU.bitwise_and)
-    tcopy(V("uof"), V("ci", 8, 24))
-    fill(V("cum", 31, None, 32), 0.0)
-    fill(V("xp"), 0.0)
-    tcopy(V("cf", 0, 4), V("ci", 1, 5))
-    PM32, ODDG, ODDP, P16, EVENG, G64, GBIG, EVENP, CA1, CA2 = [col("cf", i) for i in range(10)]
+    ts(col("ci", 4), col("ci", 0), 4, ALU.arith_shift_right, 1, ALU.bitwise_and)
+    ts(col("ci", 5), col("ci", 0), 2, ALU.arith_shift_right, 3, ALU.bitwise_and)
+    ts(col("ci", 6), col("ci", 0), 3, ALU.bitwise_and)
+    tcopy(V("cf", 0, 7), V("ci", 0, 7))
+    PP, Q16, GRP, ODDP, ODDG, Q4, B4, EVENP, SEG, E16, QC, LA, LC, K0A, K0 = [col("cf", i) for i in range(15)]
+    ts(V("ident"), V("ident"), PP, ALU.is_equal)
+    ts(V("eq"), V("eq"), Q16, ALU.is_equal)
+    tcopy(V("uof"), V("ci", 8, 16))
 
     def scorer(q, tile, p):
         quant(q, 0, tile, 0, 128)
@@ -377,188 +384,139 @@ def rank_program(g, core, T, topo):
 
     for b in range(4):
         act(V("et", 512 * b + b, 512 * b + 512, 4), V("ident"), ACT.Copy)
-    ts(V("rz0", 1, None, 8), V("i32f", 0, 160), PM32, ALU.is_gt)
-    for s in range(2, 5):
-        act(V("rz0", s, None, 8), V("et", 0, 160), ACT.Identity, bias=1.0, scale=0.0)
-    quant("s0", 80, "et", 0, 128)
-    quant("qe", 0, "et", 0, 256)
+    act(V("km"), V("eq", 0, C), ACT.Identity, bias=-BIG, scale=2.0 * BIG)
+    act(K0, col("eq", 0), ACT.Identity, bias=2.0 * BIG, scale=-5.0 * BIG)
+    act(V("k1"), V("eq", 0, C), ACT.Copy, scale=-3.0 * BIG)
     scorer("qa", "uat", "pa_")
-    for s in range(5, 8):
-        act(V("rz0", s, None, 8), V("et", 0, 160), ACT.Identity, bias=1.0, scale=0.0)
-    act(EVENG, ODDG, ACT.Identity, bias=1.0, scale=-1.0)
-    act(G64, ODDG, ACT.Copy, scale=64.0)
-    act(col("cf", 12), PM32, ACT.Identity, bias=192.0)
-    const(V("rsa"))
-    const(V("rsb0"))
-    const(V("z0", 1, None, 8))
-    const(V("rz0", 0, None, 8))
-    iota(V("jv"), [[1, C]], -(C // 2))
-    const(V("rk", 992, 1024))
-    const(V("o0"))
-    const(V("to", 0, None, 16))
-    const(V("lot", 448, 512))
-    const(V("let", 448, 512))
-    const(V("at1", 832, 896))
-    const(V("z1", 1, 1040, 5))
-    const(V("z1", 1040, 1120))
-    const(V("z1", 1121, 2160, 5))
-    const(V("z1", 2160, 2240))
-    const(V("rsb1"))
-    const(V("rsb1", 0, 3), -16)
-    const(V("rsb1", 16, 19), -16)
-    const(V("o1"))
-    iota(V("ci", 24, 52), [[128, 7], [16, 4]])
+    act(V("k1", 0, None, 16), V("eq", 0, 26), ACT.Identity, bias=K0, scale=0.0)
+    act(V("kc"), V("eq", 1, C + 1), ACT.Identity, bias=STEP, scale=-(DROP + STEP))
+    act(QC, Q16, ACT.Copy, scale=STEP + 1.0)
+    quant("qe", 0, "et", 0, 512)
+    ts(V("gst"), V("gst"), GRP, ALU.is_equal, -1.0, ALU.mult)
     quant("qx", 0, "xt", 0, 208)
     quant("qx", 208, "xt", 208, 208)
+    quant("qg", 0, "gst", 0, 128)
+    const(col("jk", JW - 1))
+    iota(V("cnt", 0, 26), [[-16, 26]], int(C - 16 - LOW - 15 * STEP))
+    iota(V("k4"), [[0, 104], [1, 4]])
+    iota(V("jv"), [[1, C]])
+    const(V("lot", C, 512))
+    const(V("let", C, 512))
     before("S", [V("xt")], [])
     dma("S", T.ubt[:], T.ub[:], [], [V("ubt")])
     dma("S", T.qwc[:].bitcast(dt.uint8), T.wc[:], [], [V("qwc")])
     dma("S", T.qws[:], T.ws[:], [], [V("qws")])
     dma("S", T.vt[:], T.v[:], [], [V("vt")])
-    quant("qe", 256, "et", 256, 256)
 
     def orders(l, state_, scorer_):
-        on_vector, cuts = ON_VECTOR[l], CUTS[l]
         n = C >> l
-        nb = (n + 31) // 32
-        w, dd = 32 * nb, nb // 2
-        S = dd + 2
-        mid = (nb + 1) // 2
-        z, rz, rsb, dw = "z%d" % l, "rz%d" % l, "rsb%d" % l, "dw%d" % l
-        mm(0, scorer_, 0, state_, 0, w)
-        mm(2, scorer_, 0, state_, 0, w)
-        mm(1, scorer_, 128, state_, 0, w)
-        mm(3, scorer_, 128, state_, 0, w)
+        nb = n // 16
+        nv = nb - 1 - ON_SCALAR[l]
+        z, qz, dw = "z%d" % l, "qz%d" % l, "dw%d" % l
+        pl = planes(nb)[0]
+        mm(0, scorer_, 0, state_, 0, n)
+        mm(1, scorer_, 0, state_, 0, n)
         for b in range(4):
             mm(4 + b, "qe", 128 * b, state_, 0, n)
 
-        def zv(e, s, k0, k1):
-            return V(z, e * w * S + k0 * S + s, e * w * S + k1 * S, S)
+        def flags(u, a, e):
+            i = nb - u
+            at = 4 * pl[i // 4][0] + i % 4
+            return V(z, at + 4 * a, at + 4 * e - 3, 4)
 
-        def scal(e, b):
-            return col("tm", e * w + 32 * b) if 32 * b + 32 <= n else col("cf", 10 + e)
+        def own(u):
+            return col("own", 16 * u + 15)
 
-        def diagonal(e):
-            tt(zv(e, 0, 0, w), ps(e, 0, w), V("tm", e * w, e * w + w), ALU.is_gt)
+        def owned(a, e):
+            scan(V("own", a, e), V("k1", a, e), V("dm", a, e), ALU.add, ALU.max)
 
-        def short(e):
-            if n < w:
-                ts(scal(e, nb - 1), col("tm", e * w + w - 32), GBIG, ALU.add)
-
-        turn(V("tm", 32 * mid, w), ps(0, 32 * mid, w))
-        turn(V("tm", 0, 32 * mid), ps(0, 0, 32 * mid))
-        short(0)
-        turn(V("tm", w, 2 * w), ps(1, 0, w))
-        diagonal(0)
-        short(1)
-        diagonal(1)
-        pcs = pieces(nb, dd)
-        later, at = [], [0]
-        for e in range(2):
-            mine = [p for p in pcs if p[0] >= on_vector[e]]
-            for b, lo, hi, wrapped, second, s in sorted(mine, key=lambda p: p[1]):
-                k0, k1 = 32 * lo, min(32 * hi, n)
-                sg = V("sg", at[0], at[0] + k1 - k0)
-                at[0] += k1 - k0
-                act(sg, ps(2 + e, k0, k1), ACT.Sign, bias=scal(e, b), scale=-1.0)
-                if len(later) > l:
-                    act(*later.pop(0))
-                acc = col(rsb if second else "rsa", 16 * e + b)
-                if wrapped:
-                    later.append((zv(e, s, k0, k1), sg, ACT.Sign, 1.0, -1.0, acc))
-                else:
-                    later.append((zv(e, s, k0, k1), sg, ACT.Relu, None, -1.0, acc))
-        while later:
-            act(*later.pop(0))
+        cut = n - FIRST[l]
+        tt(V("dm", cut, n), ps(0, cut, n), V("km", cut, n), ALU.min)
+        tt(V("dm", 0, cut // 2), ps(0, 0, cut // 2), V("km", 0, cut // 2), ALU.min)
+        owned(cut, n)
+        tt(V("dm", cut // 2, cut), ps(0, cut // 2, cut), V("km", cut // 2, cut), ALU.min)
+        owned(0, cut)
+        later = []
+        for i, u in enumerate(range(nb - 1, nv, -1)):
+            sg = V("sg", C * (i % 2), C * (i % 2) + 16 * u)
+            act(sg, ps(1, 0, 16 * u), ACT.Sign, bias=own(u), scale=-1.0)
+            if later:
+                act(*later.pop())
+            later.append((flags(u, 0, 16 * u), sg, ACT.Sign, 1.0, -1.0, col("rs", u)))
+        act(*later.pop())
         for b in range(4):
-            act(V(dw, n * b, n * b + n), ps(4 + b, 0, n), ACT.Copy, scale=0.5)
-        hl = 16 * dd
-        for e in range(2):
-            for b, lo, hi, wrapped, second, s in pcs[:on_vector[e]]:
-                ts(zv(e, s, 32 * lo, 32 * hi), ps(e, 32 * lo, 32 * hi), scal(e, b), ALU.is_gt)
-        for e in range(2):
-            for b, lo, hi, wrapped, second, s in pcs[:on_vector[e]]:
-                j = (7 * e + b) * hl
-                scan(V("jk", j, j + hl), zv(e, s, 32 * lo, 32 * lo + hl), zv(e, s, 32 * lo + hl, 32 * hi), ALU.add,
-                     ALU.add)
+            act(V(dw, b, 4 * n, 4), ps(4 + b, 0, n), ACT.Copy, scale=0.5)
+        done, queued = [], []
 
-        def columns(e, u0, u1):
-            a, b = (e * w + 32 * u0) * S, (e * w + 32 * u1) * S
-            r = 32 * u0 * S if n < w else 0
-            scan(V("zs", a, b), V(rz, r, r + b - a), V(z, a, b), ALU.mult, ALU.add)
+        def plane(k):
+            quant(qz, pl[k][0], z, pl[k][0], pl[k][1])
+            queued.append(k)
+            while queued and (done or 0 in queued):
+                j = queued.pop(queued.index(0) if 0 in queued else 0)
+                done.append(j)
+                mm(2, "qg", 0, qz, pl[j][0], pl[j][1], len(done) == 1, len(done) == len(pl))
 
-        def flip(e, u0, u1):
-            a, b = e * w + 32 * u0, e * w + 32 * u1
-            turn(V("tt", a, b), V("zs", a * S + S - 1, b * S, S))
+        tt(flags(nb, 0, n), ps(0, 0, n), V("own", 0, n), ALU.is_gt)
+        mixed = [k for k in range(len(pl)) if nb - 4 * k > nv]
+        for i, u in enumerate(range(nv, -1, -1)):
+            if u > 0:
+                ts(flags(u, 0, 16 * u), ps(0, 0, 16 * u), own(u), ALU.is_ge)
+            if u == 4:
+                scan(V("rd", 0, n), V("kr", 0, n), flags(nb, 0, n), ALU.mult, ALU.add)
+                if l == 0:
+                    ts(V("cnt", 0, 26), V("cnt", 0, 26), QC, ALU.add)
+            if i > 0:
+                v, e = u + 1, (u + 2) * JW
+                scan(V("jk", e - 8 * v, e), flags(v, 0, 8 * v), flags(v, 8 * v, 16 * v), ALU.add, ALU.add)
+                k = (nb - v) // 4
+                if k not in mixed and ((nb - v) % 4 == 3 or v == 1):
+                    plane(k)
+            for k, at in QUANT_AT[l].items():
+                if at == i:
+                    plane(k)
+        tt(V("rr", 0, nb), V("rd", 15, n, 16), V("cnt", 26 - nb, 26), ALU.add)
+        for k in mixed:
+            if k not in QUANT_AT[l]:
+                plane(k)
+        tt(V("kc", 15, 16 * (nv + 1), 16), V("jk", JW - 1, (nv + 1) * JW, JW), V("rr", 0, nv + 1), ALU.add)
+        tt(V("kc", 16 * (nv + 1) + 15, n, 16), V("rs", nv + 1, nb), V("rr", nv + 1, nb), ALU.add)
+        if l == 0:
+            ts(V("k4"), V("k4"), Q4, ALU.is_equal, -(DROP + STEP), ALU.mult)
+            act(V("k4"), V("k4"), ACT.Identity, bias=STEP)
+            act(LA, Q4, ACT.Identity, bias=-12.0 * STEP, scale=4.0 * STEP)
+            act(LC, B4, ACT.Identity, bias=LA)
+            quant("s0", 80, "et", 0, 128)
+        scan(V("xo", 0, n), ps(2, 0, n), V("kc", 0, n), ALU.max, ALU.add, -DROP)
+        pos = V("pos%d" % l, 0, nb)
+        ts(pos, V("xo", 15, n, 16), LOW, ALU.add)
+        ts(V("rw%d" % l, 0, nb), V("xo", 15, n, 16), LOW, ALU.add)
+        tcopy((V("o%d" % l), pos), V("jv", 0, n))
 
-        def fold(e, u0, u1, out, first):
-            a, b = e * w + 32 * u0, e * w + 32 * u1
-            scan(out, V("zs", a * S + 1, b * S, S), V("tt", a, b), ALU.add, ALU.subtract, first)
+    def lists(l, s0):
+        m = (104, 56)[l]
+        for s in (s0, s0 + 1):
+            scan(V("xl", m * s, m * s + m), V("k4", 0, m), V("o%d" % l, s, 4 * m, 4), ALU.add, ALU.max)
+        ts(V("ll%d" % l, m // 4 * s0, m // 4 * (s0 + 2)), V("xl", m * s0 + 3, m * (s0 + 2), 4), 4.0, ALU.mult,
+           LC, ALU.add)
 
-        last = cuts[-2]
-        for i in range(len(cuts) - 1):
-            columns(0, cuts[i], cuts[i + 1])
-            if i == 0:
-                for e in range(2):
-                    tcopy(V("rsa", 16 * e, 16 * e + on_vector[e]),
-                          V("jk", 7 * e * hl + hl - 1, (7 * e + on_vector[e]) * hl, hl))
-        columns(1, cuts[0], cuts[1])
-        flip(0, 0, nb)
-        for i in range(1, len(cuts) - 2):
-            columns(1, cuts[i], cuts[i + 1])
-        fold(0, 0, nb, V("cum", 32, 32 + w), 0.0)
-        flip(1, 0, last)
-        columns(1, last, nb)
-        fold(1, 0, last, V("cum", 544, 544 + 32 * last), 0.0)
-        m, rk, base = 16 + last, 992, col("cf", 12 + l)
-        tt(V("rsc", 0, m), V("rsa", 0, m), V(rsb, 0, m), ALU.add)
-        flip(1, last, nb)
-        for b in range(last, nb):
-            ts(col("rsc", 16 + b), col("rsa", 16 + b), col(rsb, 16 + b), ALU.add, base, ALU.add)
-        tt(V("rsc", 64, 64 + m), V("cum", 63, 63 + 32 * m, 32), V("cum", 31, 31 + 32 * m, 32), ALU.subtract)
-        ts(V("rsc", 32, 32 + m), V("rsc", 0, m), base, ALU.add)
-        for b in range(last, nb):
-            fold(1, b, b + 1, V("rk", 16 + b, 1024, 32), col("rsc", 16 + b))
-            if b == last:
-                tt(V("rk", rk, rk + m), V("rsc", 64, 64 + m), V("rsc", 32, 32 + m), ALU.add)
-        rw, o = "rw%d" % l, "o%d" % l
-        ts(V("wt", 64, 80), V("rk", rk, rk + 16), EVENG, ALU.mult)
-        turn(V("xp", 16, 48), V("rk", rk, rk + 32))
-        ts(V("wt", 80, 96), V("rk", rk + 16, rk + 32), ODDG, ALU.mult)
-        turn(V("wt", 0, 64), V("xp"))
-        tt(V(rw, 0, 2 * nb, 2), V("wt", 64, 64 + nb), V("wt", 16, 16 + nb), ALU.add)
-        tt(V(rw, 1, 2 * nb, 2), V("wt", 80, 80 + nb), V("wt", 32, 32 + nb), ALU.add)
-        t = n // 16
-        ts(V("pa", 0, t), V(rw, 0, t), 448, ALU.bitwise_and)
-        tt(V("pa", 32, 32 + t), V("pa", 0, t), V(rw, 0, t), ALU.add)
-        ts(V("pos", 0, t), V("pa", 32, 32 + t), G64, ALU.add)
-        j0 = C // 2 - n // 2
-        tcopy((V(o), V("pos", 0, t)), V("jv", j0, j0 + n))
+    def member(l, s, a, e):
+        k = (26, 14)[l] * s
+        return (V("dw%d" % l), V("ll%d" % l, k + a // 16, k + e // 16))
 
-    def lists(l, runs):
-        o, n = "o%d" % l, C >> l
-        wo = SCRATCH[o][1][1]
-        for s0, s1 in runs:
-            for s in range(s0, s1):
-                turn(V("to", 256 * s, 256 * s + wo // 4), V(o, s, wo, 4))
-        for s0, s1 in runs:
-            a, b = 256 * s0, 256 * s1
-            tt(V("wl", 8 * s0, 8 * s1), V("to", a, b, 32), V("to", a + 16, b, 32), ALU.add)
-        for s0, s1 in runs:
-            ts(V("ll%d" % l, 8 * s0, 8 * s1), V("wl", 8 * s0, 8 * s1), float(n // 2), ALU.add)
+    def second(l, odd, a, e):
+        return V("g%d" % l, (C >> l) * odd + a, (C >> l) * odd + e)
 
-    def fetch(l, odd):
-        n, k = C >> l, (7, 4)[l]
-        for b in range(4):
-            act(V("g%d" % l, 16 * k * (4 * odd + b), 16 * k * (4 * odd + b + 1)),
-                (V("dw%d" % l, n * b, n * b + n), V("ll%d" % l, 16 * odd + 8, 16 * odd + 8 + k)), ACT.Copy)
+    def pairs(l, odd, tile, first, op, a=0, e=None):
+        e = C >> l if e is None else e
+        tt(V(tile, first + a, first + e), member(l, 2 * odd, a, e), second(l, odd, a, e), op)
 
-    def pairs(l, odd, tile, first, step, op):
-        n, k = C >> l, (7, 4)[l]
-        for b in range(4):
-            tt(V(tile, first + b, 16 * k * step, step),
-               (V("dw%d" % l, n * b, n * b + n), V("ll%d" % l, 16 * odd, 16 * odd + k)),
-               V("g%d" % l, 16 * k * (4 * odd + b), 16 * k * (4 * odd + b + 1)), op)
+    def odd_lows(l):
+        n = C >> l
+        a = (128, 64)[l]
+        act(second(l, 1, a, n), member(l, 3, a, n), ACT.Copy)
+        tcopy(second(l, 1, 0, a), member(l, 3, 0, a))
+        pairs(l, 1, "lot", 0, ALU.add, 0, a)
+        pairs(l, 1, "lot", 0, ALU.add, a, n)
 
     def layer(src, a, m, tile, first, step, split):
         order = (2, 0, 3, 1) if split else range(4)
@@ -571,148 +529,143 @@ def rank_program(g, core, T, topo):
             else:
                 act(out, ps(4 + b, 0, m), ACT.Copy, scale=0.03125)
 
-    def unpack(bank, src, a, n):
-        for b in range(4):
+    def unpack(bank, src, a, n, order=range(4)):
+        for b in order:
             mm(bank + b, "qe", 128 * b, src, a, n)
 
-    def order_rows(l):
-        n = C >> l
-        act(V("olf", C * l, C * l + n), (V("o%d" % l), V("olo", 0, n // 16)), ACT.Identity, bias=float(n // 2))
-
     orders(0, "qx", "pa_")
-    act(GBIG, ODDG, ACT.Copy, scale=BIG)
-    act(EVENP, ODDP, ACT.Identity, bias=1.0, scale=-1.0)
-    act(CA1, ODDP, ACT.Identity, bias=156.0, scale=-52.0)
-    act(CA2, ODDP, ACT.Identity, bias=-156.0, scale=104.0)
-    act(col("cf", 13), PM32, ACT.Identity, bias=96.0)
-    lists(0, ((3, 4), (2, 3)))
-    fetch(0, 1)
-    pairs(0, 1, "lot", 0, 4, ALU.add)
+    lists(0, 2)
+    odd_lows(0)
     quant("s0", 0, "lot", 0, 128)
     swap_wide("s0", "r0", "h0")
-    const(V("rz1", 0, None, 5))
-    const(V("rz1", 1041, None, 5))
-    for s in range(2, 5):
-        const(V("rz1", s, None, 5), 1)
+    dma("S", T.ol[:, 0:C], T.o0[0:128:16, :], [V("o0")], [])
+    tails(1, range(4))
+    const(V("o1", 208, 224))
     const(V("ret", 256, 512))
     const(V("rot", 256, 512))
-    lists(0, ((0, 2),))
-    ts(V("olo"), V("ci", 24, 52), P16, ALU.add, G64, ALU.add)
-    fetch(0, 0)
-    order_rows(0)
-    pairs(0, 1, "ht0", 4, 8, ALU.subtract)
-    pairs(0, 0, "let", 0, 4, ALU.add)
+    const(V("ht1", 208, 512))
+    const(V("ht1", 720, 1024))
+    const(V("abe", C, 512))
+    const(V("xb"))
+    const(V("k32"), 1)
+    const(V("k32", 0, None, 32))
+    lists(0, 0)
+    act(second(0, 0, 0, C), member(0, 1, 0, C), ACT.Copy)
+    pairs(0, 1, "ht0", C, ALU.subtract)
+    pairs(0, 0, "let", 0, ALU.add)
     quant("mid0", 112, "let", 0, 128)
     layer("mid0", 112, 104, "at1", 0, 8, False)
-    pairs(0, 0, "ht0", 0, 8, ALU.subtract)
-    quant("qh0", 0, "ht0", 0, 224)
+    pairs(0, 0, "ht0", 0, ALU.subtract)
+    quant("qh0", 0, "ht0", 0, 208)
     scorer("qb", "ubt", "pb_")
-    ts(V("rz1", 1, 1040, 5), V("i32f", 0, 208), PM32, ALU.is_gt)
+    act(EVENP, ODDP, ACT.Identity, bias=1.0, scale=-1.0)
+    act(SEG, ODDP, ACT.Identity, bias=-104.0, scale=-104.0)
+    act(E16, ODDG, ACT.Copy, scale=16.0)
     unpack(0, "qh0", 0, 208)
     for b in range(4):
-        act(V("hw0", C * b, C * b + 208), ps(b, 0, 208), ACT.Copy)
-        if b < 2:
-            act(V("hw0", C * b + 208, C * b + C), ps(b, 0, 208), ACT.Copy, scale=-1.0)
-    ts(V("la", 32, 58), V("rw0", 0, 26), 1, ALU.bitwise_and)
+        for h in range(2):
+            for s in range(2):
+                act(V("hw0", C * b + 2 * h + s, C * b + C, 4), ps(b, 104 * h, 104 * h + 104), ACT.Copy,
+                    scale=1.0 - 2.0 * s)
     ts(V("la", 0, 26), V("rw0", 0, 26), 1, ALU.arith_shift_right)
+    ts(V("la", 32, 58), V("rw0", 0, 26), 5, ALU.arith_shift_right)
     quant("s1", 80, "et", 0, 128)
-    ts(V("la", 64, 90), V("la", 32, 58), 208.0, ALU.mult)
-    tcopy(V("ua0", 0, 26), V("la", 0, 26))
+    ts(V("la", 64, 90), V("la", 32, 58), 16.0, ALU.mult, E16, ALU.add)
     quant("s2", 80, "et", 0, 128)
     tt(V("la", 96, 122), V("la", 64, 90), V("la", 0, 26), ALU.add)
     quant("qv", 0, "vt", 0, 128)
-    tcopy(V("uh0", 0, 26), V("la", 96, 122))
+    tcopy(V("kk"), V("la", 96, 122))
     layer("mid0", 8, 104, "at1", 4, 8, True)
-    quant("qa1", 0, "at1", 0, 224)
+    quant("qa1", 0, "at1", 0, 208)
+
+    def signed(b):
+        act(V("hs0", b, None, 4), (V("hw0", C * b, C * b + C), V("pos0")), ACT.Copy)
 
     orders(1, "qa1", "pb_")
+    for b in range(3):
+        signed(b)
     send([(hd, V("rl", 0, 13), V("rw1", 0, 13), "hl", eng[:q4])])
-    lists(1, ((3, 4), (2, 3)))
-    fetch(1, 1)
-    pairs(1, 1, "lot", 0, 4, ALU.add)
+    lists(1, 2)
+    odd_lows(1)
     quant("s1", 0, "lot", 0, 128)
     swap_narrow("s1", "r1", "h1")
-    lists(1, ((0, 2),))
-    fetch(1, 0)
-    pairs(1, 1, "ht1", 4, 8, ALU.subtract)
-    pairs(1, 0, "let", 0, 4, ALU.add)
+    dma("S", T.ol[:, C:C + 208], T.o1[0:128:16, 0:208], [V("o1")], [])
+    lists(1, 0)
+    act(second(1, 0, 0, 208), member(1, 1, 0, 208), ACT.Copy)
+    pairs(1, 1, "ht1", 0, ALU.subtract)
+    pairs(1, 0, "let", 0, ALU.add)
+    pairs(1, 0, "ht1", 512, ALU.subtract)
     quant("mid1", 64, "let", 0, 128)
     layer("mid1", 64, 64, "ret", 0, 4, False)
-    pairs(1, 0, "ht1", 0, 8, ALU.subtract)
-    quant("qh1", 112, "ht1", 0, 128)
-    send2(hd, hc, "qh1", 112, "rh", 104, "hh")
-    quant("up1", 160, "ret", 0, 128)
-    send2(hc, hd, "up1", 160, "re_", 52, "he")
+    quant("qh1", 192, "ht1", 128, 128)
+    quant("qh1", 64, "ht1", 0, 128)
+    send2(hd, hc, "qh1", 64, "rh", 52, "hh")
 
-    def highs(a, odd, even):
+    def highs(a, h, m):
         unpack(0, "qh1", a, 128)
         for b in range(4):
-            act(V("hm", 208 * b + odd, 208 * b + odd + 52), V("ps%d" % b, 1, 104, 2), ACT.Copy)
-            act(V("hm", 208 * b + even, 208 * b + even + 52), V("ps%d" % b, 0, 104, 2), ACT.Copy)
+            act(V("hm", 156 * b + h, 156 * b + h + m), ps(b, 0, m), ACT.Copy)
 
-    def plus_minus(ab, w, a, m, bank, hw, h):
-        tt(V(ab, w + a, w + a + m), ps(bank, 0, m), V(hw, h + a, h + a + m), ALU.add)
-        tt(V(ab, w + 208 + a, w + 208 + a + m), ps(bank, 0, m), V(hw, h + a, h + a + m), ALU.subtract)
+    def put_back(src, h, tile, at):
+        unpack(4, "up1", src, 128)
+        for b in range(4):
+            for s, op in enumerate((ALU.add, ALU.subtract)):
+                tt(V(tile, at + 4 * s + b, at + C, 8), ps(4 + b, 0, 52), V("hm", 156 * b + h, 156 * b + h + 52), op)
 
-    highs(112, 0, 156)
+    def table(bank, q0, a, order, split):
+        unpack(bank, "qab", q0, 208, order)
+        for b in order:
+            out = V("dq", 4 * a + b, 4 * (a + 208), 4)
+            if split and b >= 2:
+                tcopy(out, ps(bank + b, 0, 208))
+            else:
+                act(out, ps(bank + b, 0, 208), ACT.Copy)
+
+    highs(192, 0, 52)
+    quant("up1", 112, "ret", 0, 128)
     ts(V("lb", 0, 13), V("rw1", 0, 13), EVENP, ALU.mult)
-    ts(V("lb", 16, 29), V("lst", 0, 13), ODDP, ALU.mult)
-    both = V("lb", 32, 45)
-    tt(both, V("lb", 0, 13), V("lb", 16, 29), ALU.add)
+    put_back(112, 0, "abe", 0)
+    quant("qab", 112, "abe", 0, 128)
+    send2(hc, hd, "qab", 112, "re_", 104, "he")
     layer("mid1", 12, 64, "rot", 0, 4, True)
     quant("s2", 0, "rot", 0, 128)
     swap_narrow("s2", "r2", "h2")
-    send([(p3, V("up1c", 56, 108), V("s2c", 0, 52), "a3", off[:len(off) // 2])])
-    send([(p3, V("up1s", 56, 108), V("s2s", 0, 52), "a3", off[len(off) // 2:])])
+    send([(p3, V("up1c", 60, 112), V("s2c", 0, 52), "a3", off[:len(off) // 2])])
+    send([(p3, V("up1s", 60, 112), V("s2s", 0, 52), "a3", off[len(off) // 2:])])
+    signed(3)
+    highs(12, 52, 104)
 
-    ts(V("lb", 64, 77), both, 1, ALU.bitwise_and)
-    ts(V("lb", 80, 93), both, 2, ALU.arith_shift_right)
-    ts(V("lb", 96, 109), both, 1, ALU.arith_shift_right, 1, ALU.bitwise_and)
-    tcopy(V("hs0", 0, C), (V("hw0", 0, C), V("uh0", 0, 26)))
-    act(V("hs0", C, 2 * C), (V("hw0", C, 2 * C), V("uh0", 0, 26)), ACT.Copy)
-    order_rows(1)
-    dma("S", T.ol[:], T.olf[0:128:16, :], [V("olf")], [])
-    highs(8, 52, 104)
-    ts(V("lb", 112, 125), V("lb", 64, 77), 208.0, ALU.mult, CA1, ALU.add)
-    ts(V("lb", 128, 141), V("lb", 96, 109), CA2, ALU.mult)
-    tt(V("lb", 48, 61), V("lb", 112, 125), V("lb", 80, 93), ALU.add)
-    tt(V("lb", 144, 157), V("lb", 128, 141), V("lb", 48, 61), ALU.add)
-    tcopy(V("uh1", 0, 13), V("lb", 144, 157))
-    unpack(4, "up1", 108, 128)
-    for b in range(4):
-        plus_minus("ab1", C * b, 104, 104, 4 + b, "hm", 208 * b)
-    unpack(0, "up1", 4, 128)
-    for b in (0, 3, 1, 2):
-        plus_minus("ab1", C * b, 0, 104, b, "hm", 208 * b)
-    for b in range(4):
-        out, src = V("u1t", b, None, 4), (V("ab1", C * b, C * b + C), V("uh1", 0, 13))
-        if b < 3:
-            act(out, src, ACT.Copy)
-        else:
-            tcopy(out, src)
-    quant("qu1", 0, "u1t", 0, 208)
+    ts(V("lb", 16, 29), V("lst", 0, 13), ODDP, ALU.mult)
+    both = V("lb", 32, 45)
+    tt(both, V("lb", 0, 13), V("lb", 16, 29), ALU.add)
+    ts(V("lb", 48, 61), both, 2, ALU.arith_shift_right)
+    ts(V("lb", 64, 77), both, 1, ALU.arith_shift_right, 1, ALU.bitwise_and)
+    ts(V("lb", 80, 93), V("lb", 48, 61), -2.0, ALU.mult, SEG, ALU.add)
+    ts(V("lb", 96, 109), V("lb", 64, 77), 206.0, ALU.mult)
+    tt(V("lb", 112, 125), both, V("lb", 80, 93), ALU.add)
+    tt(V("xb", 0, None, 32), V("lb", 112, 125), V("lb", 96, 109), ALU.add)
+    scan(V("rd"), V("k32"), V("xb"), ALU.mult, ALU.add)
+    turn(V("tb"), V("rd"))
+    act(V("yt"), (V("tb"), V("kk")), ACT.Identity, bias=208.0)
+    put_back(60, 52, "abl", 0)
+    scan(V("xo"), V("k4"), V("yt"), ALU.add, ALU.max)
+    put_back(8, 104, "abl", C)
+    table(0, 8, 0, range(4), False)
+    ts(V("lq"), V("xo", 3, None, 4), 4.0, ALU.mult, LC, ALU.add)
+    quant("qab", 240, "abl", 0, 208)
+    table(4, 240, 208, (2, 0, 3, 1), True)
 
-    for b in (2, 0, 3, 1):
-        mm(4 + b, "qe", 128 * b, "qu1", 0, 208)
-    for b in range(2):
-        plus_minus("ab0", C * b, 0, 208, 6 + b, "hw0", C * (2 + b))
-        act(V("da0", 208 * b, 208 * b + 208), ps(4 + b, 0, 208), ACT.Copy)
-    parts = ((0, 288), (288, C))
-    for a, e in parts:
-        for b in range(2):
-            act(V("u0t", 4 * a + 2 + b, 4 * e, 4), (V("ab0", C * b, C * b + C), V("uh0", a // 16, e // 16)), ACT.Copy)
+    parts = ((0, 144), (144, 288), (288, C))
     for h, (a, e) in enumerate(parts):
-        for b in range(2):
-            tt(V("u0t", 4 * a + b, 4 * e, 4), (V("da0", 208 * b, 208 * b + 208), V("ua0", a // 16, e // 16)),
-               V("hs0", C * b + a, C * b + e), ALU.add)
+        tt(V("u0t", 4 * a, 4 * e), (V("dq"), V("lq", a // 4, e // 4)), V("hs0", 4 * a, 4 * e), ALU.add)
         quant("qu0", a, "u0t", a, e - a)
-        mm(h, "qv", 0, "qu0", a, e - a)
+        mm(4 + h, "qv", 0, "qu0", a, e - a)
         dma("S", T.oc[:, 4 * a:4 * e], T.qu0c[:, a:e].bitcast(dt.uint8), [V("qu0c", a, e)], [])
-        if h == 1:
+        if h == len(parts) - 1:
             for k in range(4):
                 dma("S" if k < 2 else "A", T.osc[4 * k:4 * k + 4, :], T.qu0s[32 * k:32 * k + 4, :], [V("qu0s")], [])
-        act(V("yt", a, e), ps(h, 0, e - a), ACT.Copy)
-        dma("A" if h == 0 else "S", T.y[:, a:e], T.yt[:, a:e], [V("yt", a, e)], [])
+        act(V("yt", a, e), ps(4 + h, 0, e - a), ACT.Copy)
+        dma("A" if h < len(parts) - 1 else "S", T.y[:, a:e], T.yt[:, a:e], [V("yt", a, e)], [])
 
     for sem, n in count.items():
         if clock["G"].get(sem, 0) < n:

@@ -7,9 +7,10 @@ ACT = ActivationFunctionType
 C = 416
 BIG = 2.0 ** 96
 STEP, DROP, LOW = 512.0, 16384.0, 1024.0
-ON_SCALAR = (9, 3)
-QUANT_AT = ({0: 6, 1: 13}, {0: 5})
-FIRST = (32, 32)
+ON_SCALAR = (9, 4)
+QUANT_AT = ({0: 7, 1: 16}, {0: 5})
+CUTS = ((384, 192), (176, 96))
+LAG = 2
 JW = 128
 X4, U8, BF, F32, I32, U16 = "float8_e4m3fn_x4", "uint8", "bfloat16", "float32", "int32", "uint16"
 
@@ -37,8 +38,8 @@ def _mx(name, n):
 
 
 for _n, _w in (("xt", 4 * C), ("uat", 512), ("ubt", 512), ("vt", 512), ("et", 2048), ("gst", 512),
-               ("ident", 128), ("eq", 432), ("km", C), ("k1", C), ("kr", C),
-               ("k4", C), ("k32", C), ("z0", 4 * planes(26)[1]), ("z1", 4 * planes(13)[1]), ("sg", 2 * C),
+               ("ident", 128), ("gi", 128), ("eq", 432), ("km", C), ("k1", C), ("kr", C),
+               ("k4", C), ("k32", C), ("z0", 4 * planes(26)[1]), ("z1", 4 * planes(13)[1]), ("sg", 4 * C),
                ("jk", 26 * JW), ("rd", C), ("dw0", 4 * C), ("dw1", 4 * 208), ("g0", 2 * C), ("g1", C), ("lot", 512),
                ("let", 512), ("ht0", 4 * 208), ("ht1", 1024), ("at1", 4 * 208), ("ret", 512), ("rot", 512),
                ("hw0", 4 * C), ("hm", 4 * 156), ("hs0", 4 * C), ("abe", 512), ("abl", 2 * C),
@@ -355,47 +356,54 @@ def rank_program(g, core, T, topo):
             const(V("z%d" % l, 4 * (at + short), 4 * (at + w)))
 
     iota(col("ci", 0), [[0, 1]], 0, 1)
-    iota(V("ident"), [[1, 128]])
     iota(V("eq"), [[0, 27], [1, 16]])
     iota(V("ci", 8, 16), [[16, 8]])
-    iota(V("gst"), [[1, 8], [0, 64]])
+    iota(V("ident"), [[1, 128]])
+    iota(V("gi"), [[1, 8], [0, 16]])
     tails(0, (0, 2, 3, 1, 4, 5, 6))
     const(V("kr"), 1)
     const(V("kr", 0, None, 16))
-    fill(V("et"), 0.0)
+    fill(V("et", 0, 512), 0.0)
     ts(col("ci", 1), col("ci", 0), 15, ALU.bitwise_and)
     ts(col("ci", 2), col("ci", 0), 4, ALU.arith_shift_right)
     ts(col("ci", 3), col("ci", 0), 1, ALU.bitwise_and)
     ts(col("ci", 4), col("ci", 0), 4, ALU.arith_shift_right, 1, ALU.bitwise_and)
     ts(col("ci", 5), col("ci", 0), 2, ALU.arith_shift_right, 3, ALU.bitwise_and)
     ts(col("ci", 6), col("ci", 0), 3, ALU.bitwise_and)
+    fill(V("et", 512, 1024), 0.0)
     tcopy(V("cf", 0, 7), V("ci", 0, 7))
-    PP, Q16, GRP, ODDP, ODDG, Q4, B4, EVENP, SEG, E16, QC, LA, LC, K0A, K0 = [col("cf", i) for i in range(15)]
-    ts(V("ident"), V("ident"), PP, ALU.is_equal)
+    PP, Q16, GRP, ODDP, ODDG, Q4, B4, EVENP, SEG, E16, QC, LA, LC, K0 = [col("cf", i) for i in range(14)]
+    fill(V("et", 1024, 1536), 0.0)
     ts(V("eq"), V("eq"), Q16, ALU.is_equal)
     tcopy(V("uof"), V("ci", 8, 16))
+    fill(V("et", 1536, 2048), 0.0)
 
-    def scorer(q, tile, p):
-        quant(q, 0, tile, 0, 128)
+    def pick_codes(q, p):
         src, dst, lst = V(q + "c"), V(p + "c"), V("uof")
         run("V", [src, lst], [dst], lambda: g.vector.tensor_copy(
             ap(dst).bitcast(dt.uint32), ap(src).bitcast(dt.uint32).indirect(ap(lst))))
-        act(V(p + "s"), (V(q + "s"), lst), ACT.Copy)
 
-    for b in range(4):
-        act(V("et", 512 * b + b, 512 * b + 512, 4), V("ident"), ACT.Copy)
-    act(V("km"), V("eq", 0, C), ACT.Identity, bias=-BIG, scale=2.0 * BIG)
+    def pick_scales(q, p):
+        act(V(p + "s"), (V(q + "s"), V("uof")), ACT.Copy)
+
     act(K0, col("eq", 0), ACT.Identity, bias=2.0 * BIG, scale=-5.0 * BIG)
     act(V("k1"), V("eq", 0, C), ACT.Copy, scale=-3.0 * BIG)
-    scorer("qa", "uat", "pa_")
+    act(V("km"), V("eq", 0, C), ACT.Identity, bias=-BIG, scale=2.0 * BIG)
     act(V("k1", 0, None, 16), V("eq", 0, 26), ACT.Identity, bias=K0, scale=0.0)
+    ts(V("ident"), V("ident"), PP, ALU.is_equal)
+    quant("qa", 0, "uat", 0, 128)
+    pick_scales("qa", "pa_")
+    for b in range(4):
+        act(V("et", 512 * b + b, 512 * b + 512, 4), V("ident"), ACT.Copy)
+    pick_codes("qa", "pa_")
+    for b in range(4):
+        ts(V("gst", b, None, 4), V("gi"), GRP, ALU.is_equal, -1.0, ALU.mult)
     act(V("kc"), V("eq", 1, C + 1), ACT.Identity, bias=STEP, scale=-(DROP + STEP))
     act(QC, Q16, ACT.Copy, scale=STEP + 1.0)
-    quant("qe", 0, "et", 0, 512)
-    ts(V("gst"), V("gst"), GRP, ALU.is_equal, -1.0, ALU.mult)
     quant("qx", 0, "xt", 0, 208)
-    quant("qx", 208, "xt", 208, 208)
     quant("qg", 0, "gst", 0, 128)
+    quant("qx", 208, "xt", 208, 208)
+    quant("qe", 0, "et", 0, 512)
     const(col("jk", JW - 1))
     iota(V("cnt", 0, 26), [[-16, 26]], int(C - 16 - LOW - 15 * STEP))
     iota(V("k4"), [[0, 104], [1, 4]])
@@ -430,15 +438,19 @@ def rank_program(g, core, T, topo):
         def owned(a, e):
             scan(V("own", a, e), V("k1", a, e), V("dm", a, e), ALU.add, ALU.max)
 
-        cut = n - FIRST[l]
-        tt(V("dm", cut, n), ps(0, cut, n), V("km", cut, n), ALU.min)
-        tt(V("dm", 0, cut // 2), ps(0, 0, cut // 2), V("km", 0, cut // 2), ALU.min)
-        owned(cut, n)
-        tt(V("dm", cut // 2, cut), ps(0, cut // 2, cut), V("km", cut // 2, cut), ALU.min)
-        owned(0, cut)
+        def masked(a, e):
+            tt(V("dm", a, e), ps(0, a, e), V("km", a, e), ALU.min)
+
+        hi, mid = CUTS[l]
+        masked(hi, n)
+        masked(mid, hi)
+        owned(hi, n)
+        masked(0, mid)
+        owned(mid, hi)
+        owned(0, mid)
         later = []
         for i, u in enumerate(range(nb - 1, nv, -1)):
-            sg = V("sg", C * (i % 2), C * (i % 2) + 16 * u)
+            sg = V("sg", C * (i % 4), C * (i % 4) + 16 * u)
             act(sg, ps(1, 0, 16 * u), ACT.Sign, bias=own(u), scale=-1.0)
             if later:
                 act(*later.pop())
@@ -456,17 +468,21 @@ def rank_program(g, core, T, topo):
                 done.append(j)
                 mm(2, "qg", 0, qz, pl[j][0], pl[j][1], len(done) == 1, len(done) == len(pl))
 
-        tt(flags(nb, 0, n), ps(0, 0, n), V("own", 0, n), ALU.is_gt)
         mixed = [k for k in range(len(pl)) if nb - 4 * k > nv]
-        for i, u in enumerate(range(nv, -1, -1)):
+        for i, u in enumerate(range(nv, -LAG, -1)):
             if u > 0:
                 ts(flags(u, 0, 16 * u), ps(0, 0, 16 * u), own(u), ALU.is_ge)
-            if u == 4:
+            if i == 0:
+                tt(flags(nb, 0, n), ps(0, 0, n), V("own", 0, n), ALU.is_gt)
+            if u == 5:
                 scan(V("rd", 0, n), V("kr", 0, n), flags(nb, 0, n), ALU.mult, ALU.add)
                 if l == 0:
                     ts(V("cnt", 0, 26), V("cnt", 0, 26), QC, ALU.add)
-            if i > 0:
-                v, e = u + 1, (u + 2) * JW
+            if u == 1:
+                tt(V("rr", 0, nb), V("rd", 15, n, 16), V("cnt", 26 - nb, 26), ALU.add)
+            if i >= LAG:
+                v = u + LAG
+                e = (v + 1) * JW
                 scan(V("jk", e - 8 * v, e), flags(v, 0, 8 * v), flags(v, 8 * v, 16 * v), ALU.add, ALU.add)
                 k = (nb - v) // 4
                 if k not in mixed and ((nb - v) % 4 == 3 or v == 1):
@@ -474,28 +490,33 @@ def rank_program(g, core, T, topo):
             for k, at in QUANT_AT[l].items():
                 if at == i:
                     plane(k)
-        tt(V("rr", 0, nb), V("rd", 15, n, 16), V("cnt", 26 - nb, 26), ALU.add)
         for k in mixed:
             if k not in QUANT_AT[l]:
                 plane(k)
         tt(V("kc", 15, 16 * (nv + 1), 16), V("jk", JW - 1, (nv + 1) * JW, JW), V("rr", 0, nv + 1), ALU.add)
         tt(V("kc", 16 * (nv + 1) + 15, n, 16), V("rs", nv + 1, nb), V("rr", nv + 1, nb), ALU.add)
-        if l == 0:
-            ts(V("k4"), V("k4"), Q4, ALU.is_equal, -(DROP + STEP), ALU.mult)
-            act(V("k4"), V("k4"), ACT.Identity, bias=STEP)
-            act(LA, Q4, ACT.Identity, bias=-12.0 * STEP, scale=4.0 * STEP)
-            act(LC, B4, ACT.Identity, bias=LA)
-            quant("s0", 80, "et", 0, 128)
+        spare()
         scan(V("xo", 0, n), ps(2, 0, n), V("kc", 0, n), ALU.max, ALU.add, -DROP)
+        spare()
         pos = V("pos%d" % l, 0, nb)
         ts(pos, V("xo", 15, n, 16), LOW, ALU.add)
         ts(V("rw%d" % l, 0, nb), V("xo", 15, n, 16), LOW, ALU.add)
+        spare()
         tcopy((V("o%d" % l), pos), V("jv", 0, n))
+        spare()
+
+    waiting = []
+
+    def spare():
+        if waiting:
+            waiting.pop(0)()
+
+    def picked(l, s):
+        m = (104, 56)[l]
+        scan(V("xl", m * s, m * s + m), V("k4", 0, m), V("o%d" % l, s, 4 * m, 4), ALU.add, ALU.max)
 
     def lists(l, s0):
         m = (104, 56)[l]
-        for s in (s0, s0 + 1):
-            scan(V("xl", m * s, m * s + m), V("k4", 0, m), V("o%d" % l, s, 4 * m, 4), ALU.add, ALU.max)
         ts(V("ll%d" % l, m // 4 * s0, m // 4 * (s0 + 2)), V("xl", m * s0 + 3, m * (s0 + 2), 4), 4.0, ALU.mult,
            LC, ALU.add)
 
@@ -513,93 +534,108 @@ def rank_program(g, core, T, topo):
     def odd_lows(l):
         n = C >> l
         a = (128, 64)[l]
+        picked(l, 3)
+        picked(l, 2)
+        picked(l, 1)
+        lists(l, 2)
+        picked(l, 0)
         act(second(l, 1, a, n), member(l, 3, a, n), ACT.Copy)
         tcopy(second(l, 1, 0, a), member(l, 3, 0, a))
+        lists(l, 0)
+        act(second(l, 0, 0, n), member(l, 1, 0, n), ACT.Copy)
+        spare()
         pairs(l, 1, "lot", 0, ALU.add, 0, a)
         pairs(l, 1, "lot", 0, ALU.add, a, n)
+        spare()
 
     def layer(src, a, m, tile, first, step, split):
-        order = (2, 0, 3, 1) if split else range(4)
+        order, bank = ((2, 0, 3, 1), 4) if split else (range(4), 0)
         for b in order:
-            mm(4 + b, "qw", 128 * b, src, a, 128)
+            mm(bank + b, "qw", 128 * b, src, a, 128)
         for b in order:
             out = V(tile, first + b, step * m, step)
             if split and b >= 2:
-                ts(out, ps(4 + b, 0, m), 0.03125, ALU.mult)
+                ts(out, ps(bank + b, 0, m), 0.03125, ALU.mult)
             else:
-                act(out, ps(4 + b, 0, m), ACT.Copy, scale=0.03125)
+                act(out, ps(bank + b, 0, m), ACT.Copy, scale=0.03125)
 
     def unpack(bank, src, a, n, order=range(4)):
         for b in order:
             mm(bank + b, "qe", 128 * b, src, a, n)
 
-    orders(0, "qx", "pa_")
-    lists(0, 2)
-    odd_lows(0)
-    quant("s0", 0, "lot", 0, 128)
-    swap_wide("s0", "r0", "h0")
-    dma("S", T.ol[:, 0:C], T.o0[0:128:16, :], [V("o0")], [])
+    def list_constants():
+        ts(V("k4"), V("k4"), Q4, ALU.is_equal, -(DROP + STEP), ALU.mult)
+        act(V("k4"), V("k4"), ACT.Identity, bias=STEP)
+        act(LA, Q4, ACT.Identity, bias=-12.0 * STEP, scale=4.0 * STEP)
+        act(E16, ODDG, ACT.Copy, scale=16.0)
+        act(EVENP, ODDP, ACT.Identity, bias=1.0, scale=-1.0)
+        act(LC, B4, ACT.Identity, bias=LA)
+        act(SEG, ODDP, ACT.Identity, bias=-104.0, scale=-104.0)
+        quant("s0", 80, "et", 0, 128)
+
     tails(1, range(4))
     const(V("o1", 208, 224))
     const(V("ret", 256, 512))
     const(V("rot", 256, 512))
     const(V("ht1", 208, 512))
+    waiting += [list_constants,
+                lambda: (quant("qb", 0, "ubt", 0, 128), pick_scales("qb", "pb_")),
+                lambda: quant("s1", 80, "et", 0, 128),
+                lambda: pick_codes("qb", "pb_"),
+                lambda: (ts(V("la", 0, 26), V("rw0", 0, 26), 1, ALU.arith_shift_right),
+                         ts(V("la", 32, 58), V("rw0", 0, 26), 5, ALU.arith_shift_right)),
+                lambda: pairs(0, 1, "ht0", C, ALU.subtract, 0, 96)]
+    orders(0, "qx", "pa_")
+    odd_lows(0)
+    quant("s0", 0, "lot", 0, 128)
+    swap_wide("s0", "r0", "h0")
+    dma("S", T.ol[:, 0:C], T.o0[0:128:16, :], [V("o0")], [])
     const(V("ht1", 720, 1024))
     const(V("abe", C, 512))
     const(V("xb"))
     const(V("k32"), 1)
     const(V("k32", 0, None, 32))
-    lists(0, 0)
-    act(second(0, 0, 0, C), member(0, 1, 0, C), ACT.Copy)
-    pairs(0, 1, "ht0", C, ALU.subtract)
     pairs(0, 0, "let", 0, ALU.add)
+    ts(V("la", 64, 90), V("la", 32, 58), 16.0, ALU.mult, E16, ALU.add)
+    quant("qv", 0, "vt", 0, 128)
     quant("mid0", 112, "let", 0, 128)
     layer("mid0", 112, 104, "at1", 0, 8, False)
-    pairs(0, 0, "ht0", 0, ALU.subtract)
-    quant("qh0", 0, "ht0", 0, 208)
-    scorer("qb", "ubt", "pb_")
-    act(EVENP, ODDP, ACT.Identity, bias=1.0, scale=-1.0)
-    act(SEG, ODDP, ACT.Identity, bias=-104.0, scale=-104.0)
-    act(E16, ODDG, ACT.Copy, scale=16.0)
-    unpack(0, "qh0", 0, 208)
-    for b in range(4):
-        for h in range(2):
-            for s in range(2):
-                act(V("hw0", C * b + 2 * h + s, C * b + C, 4), ps(b, 104 * h, 104 * h + 104), ACT.Copy,
-                    scale=1.0 - 2.0 * s)
-    ts(V("la", 0, 26), V("rw0", 0, 26), 1, ALU.arith_shift_right)
-    ts(V("la", 32, 58), V("rw0", 0, 26), 5, ALU.arith_shift_right)
-    quant("s1", 80, "et", 0, 128)
-    ts(V("la", 64, 90), V("la", 32, 58), 16.0, ALU.mult, E16, ALU.add)
-    quant("s2", 80, "et", 0, 128)
     tt(V("la", 96, 122), V("la", 64, 90), V("la", 0, 26), ALU.add)
-    quant("qv", 0, "vt", 0, 128)
+    pairs(0, 1, "ht0", C, ALU.subtract, 96, C)
+    pairs(0, 0, "ht0", 0, ALU.subtract)
     tcopy(V("kk"), V("la", 96, 122))
+    quant("s2", 80, "et", 0, 128)
+    quant("qh0", 0, "ht0", 0, 208)
     layer("mid0", 8, 104, "at1", 4, 8, True)
     quant("qa1", 0, "at1", 0, 208)
 
     def signed(b):
         act(V("hs0", b, None, 4), (V("hw0", C * b, C * b + C), V("pos0")), ACT.Copy)
 
+    def highs_by_place(bs):
+        unpack(4, "qh0", 0, 208, bs)
+        for b in bs:
+            for h in range(2):
+                for s in range(2):
+                    act(V("hw0", C * b + 2 * h + s, C * b + C, 4), ps(4 + b, 104 * h, 104 * h + 104), ACT.Copy,
+                        scale=1.0 - 2.0 * s)
+
+    waiting += [lambda: highs_by_place(range(3)), lambda: 0, lambda: 0, lambda: ts(V("lb", 0, 13), V("rw1", 0, 13), EVENP, ALU.mult),
+                lambda: 0, lambda: pairs(1, 1, "ht1", 0, ALU.subtract, 0, 96)]
     orders(1, "qa1", "pb_")
-    for b in range(3):
-        signed(b)
     send([(hd, V("rl", 0, 13), V("rw1", 0, 13), "hl", eng[:q4])])
-    lists(1, 2)
     odd_lows(1)
     quant("s1", 0, "lot", 0, 128)
     swap_narrow("s1", "r1", "h1")
     dma("S", T.ol[:, C:C + 208], T.o1[0:128:16, 0:208], [V("o1")], [])
-    lists(1, 0)
-    act(second(1, 0, 0, 208), member(1, 1, 0, 208), ACT.Copy)
-    pairs(1, 1, "ht1", 0, ALU.subtract)
+    highs_by_place((3,))
+    signed(0)
     pairs(1, 0, "let", 0, ALU.add)
-    pairs(1, 0, "ht1", 512, ALU.subtract)
+    pairs(1, 0, "ht1", 512, ALU.subtract, 0, 96)
     quant("mid1", 64, "let", 0, 128)
     layer("mid1", 64, 64, "ret", 0, 4, False)
-    quant("qh1", 192, "ht1", 128, 128)
-    quant("qh1", 64, "ht1", 0, 128)
-    send2(hd, hc, "qh1", 64, "rh", 52, "hh")
+    pairs(1, 0, "ht1", 512, ALU.subtract, 96, 208)
+    pairs(1, 1, "ht1", 0, ALU.subtract, 96, 208)
 
     def highs(a, h, m):
         unpack(0, "qh1", a, 128)
@@ -621,43 +657,52 @@ def rank_program(g, core, T, topo):
             else:
                 act(out, ps(bank + b, 0, 208), ACT.Copy)
 
+    both = V("lb", 32, 45)
+    quant("qh1", 192, "ht1", 128, 128)
     highs(192, 0, 52)
     quant("up1", 112, "ret", 0, 128)
-    ts(V("lb", 0, 13), V("rw1", 0, 13), EVENP, ALU.mult)
+    quant("qh1", 64, "ht1", 0, 128)
+    send2(hd, hc, "qh1", 64, "rh", 52, "hh")
+    ts(V("lb", 16, 29), V("lst", 0, 13), ODDP, ALU.mult)
     put_back(112, 0, "abe", 0)
+    tt(both, V("lb", 0, 13), V("lb", 16, 29), ALU.add)
+    layer("mid1", 12, 64, "rot", 0, 4, False)
     quant("qab", 112, "abe", 0, 128)
     send2(hc, hd, "qab", 112, "re_", 104, "he")
-    layer("mid1", 12, 64, "rot", 0, 4, True)
+    ts(V("lb", 48, 61), both, 2, ALU.arith_shift_right)
+    ts(V("lb", 64, 77), both, 1, ALU.arith_shift_right, 1, ALU.bitwise_and)
     quant("s2", 0, "rot", 0, 128)
     swap_narrow("s2", "r2", "h2")
     send([(p3, V("up1c", 60, 112), V("s2c", 0, 52), "a3", off[:len(off) // 2])])
     send([(p3, V("up1s", 60, 112), V("s2s", 0, 52), "a3", off[len(off) // 2:])])
-    signed(3)
-    highs(12, 52, 104)
-
-    ts(V("lb", 16, 29), V("lst", 0, 13), ODDP, ALU.mult)
-    both = V("lb", 32, 45)
-    tt(both, V("lb", 0, 13), V("lb", 16, 29), ALU.add)
-    ts(V("lb", 48, 61), both, 2, ALU.arith_shift_right)
-    ts(V("lb", 64, 77), both, 1, ALU.arith_shift_right, 1, ALU.bitwise_and)
+    signed(1)
+    signed(2)
     ts(V("lb", 80, 93), V("lb", 48, 61), -2.0, ALU.mult, SEG, ALU.add)
     ts(V("lb", 96, 109), V("lb", 64, 77), 206.0, ALU.mult)
     tt(V("lb", 112, 125), both, V("lb", 80, 93), ALU.add)
     tt(V("xb", 0, None, 32), V("lb", 112, 125), V("lb", 96, 109), ALU.add)
     scan(V("rd"), V("k32"), V("xb"), ALU.mult, ALU.add)
     turn(V("tb"), V("rd"))
+    highs(12, 52, 104)
     act(V("yt"), (V("tb"), V("kk")), ACT.Identity, bias=208.0)
+    signed(3)
     put_back(60, 52, "abl", 0)
-    scan(V("xo"), V("k4"), V("yt"), ALU.add, ALU.max)
     put_back(8, 104, "abl", C)
+    scan(V("xo"), V("k4"), V("yt"), ALU.add, ALU.max)
+    quant("qab", 240, "abl", 0, 208)
     table(0, 8, 0, range(4), False)
     ts(V("lq"), V("xo", 3, None, 4), 4.0, ALU.mult, LC, ALU.add)
-    quant("qab", 240, "abl", 0, 208)
     table(4, 240, 208, (2, 0, 3, 1), True)
 
     parts = ((0, 144), (144, 288), (288, C))
-    for h, (a, e) in enumerate(parts):
+
+    def gather(a, e):
         tt(V("u0t", 4 * a, 4 * e), (V("dq"), V("lq", a // 4, e // 4)), V("hs0", 4 * a, 4 * e), ALU.add)
+
+    gather(*parts[0])
+    for h, (a, e) in enumerate(parts):
+        if h != 1:
+            gather(*parts[max(h, 1)])
         quant("qu0", a, "u0t", a, e - a)
         mm(4 + h, "qv", 0, "qu0", a, e - a)
         dma("S", T.oc[:, 4 * a:4 * e], T.qu0c[:, a:e].bitcast(dt.uint8), [V("qu0c", a, e)], [])

import numpy as np
from concourse.bass import DstId, RemoteDMATransfer
from concourse.mybir import dt, AluOpType, ActivationFunctionType

ALU = AluOpType
ACT = ActivationFunctionType
C = 416
BIG = 2.0 ** 96
STEP, DROP, LOW = 512.0, 16384.0, 1024.0
ON_SCALAR = (9, 4)
QUANT_AT = ({0: 7, 1: 16}, {0: 5})
CUTS = ((384, 192), (176, 96))
LAG = 2
JW = 128
X4, U8, BF, F32, I32, U16 = "float8_e4m3fn_x4", "uint8", "bfloat16", "float32", "int32", "uint16"


def planes(nb):
    lens = [16 * (nb - i) for i in range(nb)]
    out, at = [], 0
    for k in range(0, nb, 4):
        w = max(128, lens[k])
        out.append((at, w, lens[k + 3] if k + 3 < nb else 0))
        at += w
    return out, at


SCRATCH = {}


def _buf(name, n, dtype):
    SCRATCH[name] = ("sbuf", [128, n], dtype)


def _mx(name, n):
    _buf(name + "c", n, X4)
    _buf(name + "s", n, U8)


for _n, _w in (("xt", 4 * C), ("uat", 512), ("ubt", 512), ("vt", 512), ("et", 2048), ("gst", 512),
               ("ident", 128), ("gi", 128), ("eq", 432), ("km", C), ("k1", C), ("kr", C),
               ("k4", C), ("k32", C), ("z0", 4 * planes(26)[1]), ("z1", 4 * planes(13)[1]), ("sg", 4 * C),
               ("jk", 26 * JW), ("rd", C), ("dw0", 4 * C), ("dw1", 4 * 208), ("g0", 2 * C), ("g1", C), ("lot", 512),
               ("let", 512), ("ht0", 4 * 208), ("ht1", 1024), ("at1", 4 * 208), ("ret", 512), ("rot", 512),
               ("hw0", 4 * C), ("hm", 4 * 156), ("hs0", 4 * C), ("abe", 512), ("abl", 2 * C),
               ("dq", 4 * C), ("xb", C), ("tb", C), ("u0t", 4 * C)):
    _buf(_n, _w, BF)
for _n, _w in (("kc", C), ("dm", C), ("own", C), ("xo", C), ("rs", 32), ("rr", 32), ("cnt", 32), ("cf", 24), ("jv", C),
               ("o0", C), ("o1", 224), ("xl", C), ("yt", C)):
    _buf(_n, _w, F32)
for _n, _w in (("ci", 24), ("rw0", 28), ("rw1", 16), ("la", 128), ("lb", 128), ("lst", 16), ("rl", 16)):
    _buf(_n, _w, I32)
for _n, _w in (("uof", 8), ("pos0", 26), ("pos1", 14), ("ll0", 104), ("ll1", 56), ("kk", 26), ("lq", 104)):
    _buf(_n, _w, U16)
for _n, _w in (("qx", C), ("qa", 128), ("qb", 128), ("qv", 128), ("pa_", 128), ("pb_", 128), ("qe", 512), ("qw", 512),
               ("qg", 128), ("qz0", planes(26)[1]), ("qz1", planes(13)[1]), ("s0", 208), ("s1", 208), ("s2", 208),
               ("mid0", 240), ("mid1", 192), ("qa1", 208), ("qh0", 208), ("qh1", 320), ("up1", 240), ("qab", 448),
               ("qu0", C)):
    _mx(_n, _w)
for _n, _w, _v in (("r0", 52, 208), ("r1", 52, 208), ("r2", 52, 208), ("rh", 52, 52), ("re_", 104, 104)):
    _buf(_n + "c", _w, X4)
    _buf(_n + "s", _v, U8)
for _k in range(8):
    SCRATCH["ps%d" % _k] = ("psum", [128, 512], F32)

NDMA = 24
SEMAPHORES = (["cV", "cA", "cP", "cG", "sent", "a0", "a1", "a2", "a3", "ah", "ae", "al", "h0", "h1", "h2", "hh", "he",
               "hl"] + ["d%d" % _k for _k in range(NDMA)])


def bits(engines):
    m = 0
    for e in engines:
        m |= 1 << e
    return m


def helpers(core, far, topo):
    ok = [c for c in topo.cores_of(core) if c != core and topo.may_write(c, far)]
    near = [c for c in ok if topo.die(c) == topo.die(core)]
    other = [c for c in ok if topo.die(c) != topo.die(core)]
    return near[0], near[1], other[0], other[1]


def relay_program(g, core, T, topo, r):
    me = T.cores[r]
    p1, p2 = T.cores[r ^ 1], T.cores[r ^ 2]
    ha, hb, hc, hd = helpers(me, p1, topo)
    quarter = len(topo.engines(me, core)) // 4
    total = [0]

    def on(dst, out, in_, sem):
        rid, pid = topo.addr(dst, core)
        e = topo.engines(core, dst)
        g.remote_dma(out, in_, T.sem[sem], T.sem.sent, pid, rid, bits(e))
        total[0] += len(e)

    def cod(name, a, b):
        return T[name][:, a:b].bitcast(dt.uint8)

    if core == ha:
        g.wait_ge(T.sem.h0, quarter)
        on(p1, cod("mid0c", 8, 60), cod("r0c", 0, 52), "a0")
        g.wait_ge(T.sem.h1, 2 * quarter)
        on(p2, cod("mid1c", 12, 64), cod("r1c", 0, 52), "a1")
        g.wait_ge(T.sem.h2, 2 * quarter)
        on(p2, cod("up1c", 8, 60), cod("r2c", 0, 52), "a2")
    elif core == hb:
        g.wait_ge(T.sem.h0, quarter)
        on(p1, T.mid0s[:, 8:112], T.r0s[:, 0:104], "a0")
        g.wait_ge(T.sem.h1, 2 * quarter)
        on(p2, T.mid1s[:, 12:64], T.r1s[:, 0:52], "a1")
        g.wait_ge(T.sem.h2, 2 * quarter)
        on(p2, T.up1s[:, 8:60], T.r2s[:, 0:52], "a2")
    elif core == hc:
        g.wait_ge(T.sem.h0, quarter)
        on(p1, cod("mid0c", 60, 112), cod("r0c", 0, 52), "a0")
        g.wait_ge(T.sem.hh, 2 * quarter)
        on(p1, T.qh1s[:, 12:64], T.rhs[:, 0:52], "ah")
        g.wait_ge(T.sem.he, 2 * quarter)
        on(p1, cod("qabc", 8, 112), cod("re_c", 0, 104), "ae")
    elif core == hd:
        g.wait_ge(T.sem.hl, quarter)
        on(p1, T.lst[:, 0:13], T.rl[:, 0:13], "al")
        g.wait_ge(T.sem.hh, 2 * quarter)
        on(p1, cod("qh1c", 12, 64), cod("rhc", 0, 52), "ah")
        g.wait_ge(T.sem.he, 2 * quarter)
        on(p1, T.qabs[:, 8:112], T.re_s[:, 0:104], "ae")
    if total[0]:
        g.wait_ge(T.sem.sent, total[0])


def rank_program(g, core, T, topo):
    rank = T.rank_of(core)
    if rank is None:
        for r, c in enumerate(T.cores):
            if core in topo.cores_of(c):
                relay_program(g, core, T, topo, r)
        return
    p1, p3 = T.cores[rank ^ 1], T.cores[rank ^ 3]
    ha, hb, hc, hd = helpers(core, p1, topo)

    queue = {"V": g.vector, "A": g.scalar, "P": g.tensor, "G": g, "S": g.sync}
    clock = {q: {} for q in queue}
    count = {}
    toks = [None]
    wr, rd = {}, {}

    def cols(v):
        return slice(v[1], v[2], v[3])

    def state(name):
        if name not in wr:
            n = SCRATCH[name][1][1]
            wr[name] = np.zeros(n, np.int64)
            rd[name] = {}
        return wr[name], rd[name]

    def wait(q, tid):
        sem, n, seen = toks[tid]
        if clock[q].get(sem, 0) >= n:
            return
        queue[q].wait_ge(T.sem[sem], n)
        for s, k in seen.items():
            if clock[q].get(s, 0) < k:
                clock[q][s] = k
        clock[q][sem] = n

    def before(q, reads, writes):
        need = set()
        for v in reads:
            w, r = state(v[0])
            bank = v[0].startswith("ps")
            need.update(np.unique(w if bank else w[cols(v)]).tolist())
            if bank:
                for who, a in r.items():
                    if who != q:
                        need.update(np.unique(a).tolist())
        for v in writes:
            w, r = state(v[0])
            s = slice(None) if v[0].startswith("ps") else cols(v)
            need.update(np.unique(w[s]).tolist())
            for a in r.values():
                need.update(np.unique(a[s]).tolist())
        need.discard(0)
        for tid in sorted(need, reverse=True):
            wait(q, tid)

    def after(who, tok, reads, writes):
        toks.append(tok)
        tid = len(toks) - 1
        for v in reads:
            w, r = state(v[0])
            if who not in r:
                r[who] = np.zeros(len(w), np.int64)
            r[who][cols(v)] = tid
        for v in writes:
            state(v[0])[0][cols(v)] = tid
        return tid

    def run(q, reads, writes, call, adds=False):
        before(q, reads, [] if adds else writes)
        sem = "c" + q
        count[sem] = count.get(sem, 0) + 1
        call().then_inc(T.sem[sem], 1)
        return after(q, (sem, count[sem], dict(clock[q])), reads, writes)

    ndma = [0]

    def dma(q, out, in_, reads, writes):
        before(q, reads, writes)
        sem = "d%d" % ndma[0]
        ndma[0] += 1
        count[sem] = 16
        queue[q].dma_start(out, in_).then_inc(T.sem[sem], 16)
        return after(sem, (sem, 16, dict(clock[q])), reads, writes)

    def lands(sem, n, writes):
        count[sem] = n
        after(sem, (sem, n, {}), [], writes)

    def V(name, a=0, b=None, s=1):
        return (name, a, SCRATCH[name][1][1] if b is None else b, s)

    def col(name, a):
        return (name, a, a + 1, 1)

    def ap(v):
        if not isinstance(v, tuple):
            return v
        if len(v) == 2:
            return ap(v[0]).indirect(ap(v[1]))
        if v[3] == 1:
            return T[v[0]][:, v[1]:v[2]]
        return T[v[0]][:, v[1]:v[2]:v[3]]

    def named(*vs):
        out = []
        for v in vs:
            if isinstance(v, tuple):
                out.extend(v if len(v) == 2 else [v])
        return out

    def tcopy(out, in_):
        if len(out) == 2:
            return run("V", named(in_, out[1]), [out[0]], lambda: g.vector.tensor_copy(ap(out), ap(in_)))
        return run("V", named(in_), [out], lambda: g.vector.tensor_copy(ap(out), ap(in_)))

    def tt(out, a, b, op):
        return run("V", named(a, b), [out], lambda: g.vector.tensor_tensor(ap(out), ap(a), ap(b), op))

    def ts(out, a, s1, op0, s2=None, op1=None):
        if op1 is None:
            return run("V", named(a, s1), [out], lambda: g.vector.tensor_scalar(ap(out), ap(a), ap(s1), None, op0))
        return run("V", named(a, s1, s2), [out],
                   lambda: g.vector.tensor_scalar(ap(out), ap(a), ap(s1), ap(s2), op0, op1))

    def scan(out, a, b, op0, op1, first=0.0):
        return run("V", named(a, b, first), [out],
                   lambda: g.vector.tensor_tensor_scan(ap(out), ap(a), ap(b), ap(first), op0, op1))

    def turn(out, a):
        return run("V", [a], [out], lambda: g.vector.transpose(ap(out), ap(a)))

    def fill(out, c):
        return run("V", [], [out], lambda: g.vector.memset(ap(out), c))

    def act(out, a, func, bias=None, scale=None, accum=None):
        kw = {}
        if bias is not None:
            kw["bias"] = ap(bias)
        if scale is not None:
            kw["scale"] = scale
        if accum is not None:
            kw["accum_out"] = ap(accum)
        return run("A", named(a, bias), named(out, accum), lambda: g.scalar.activation(ap(out), ap(a), func, **kw))

    def iota(out, pattern, base=0, cm=0):
        if SCRATCH[out[0]][2] == I32:
            return run("G", [], [out], lambda: g.iota(ap(out), pattern, base, cm))
        return run("G", [], [out], lambda: g.iota(ap(out), pattern, base, cm, allow_small_or_imprecise_dtypes=True))

    def const(out, c=0):
        return iota(out, [[0, len(range(out[1], out[2], out[3]))]], c)

    def quant(name, a, tile, t0, n):
        c, s, t = V(name + "c", a, a + n), V(name + "s", a, a + n), V(tile, 4 * t0, 4 * (t0 + n))
        return run("V", [t], [c, s], lambda: g.vector.quantize_mx(ap(c), ap(s), ap(t)))

    def mm(bank, w, w0, x, x0, n, start=True, stop=True):
        vs = [V(w + "c", w0, w0 + 128), V(w + "s", w0, w0 + 128), V(x + "c", x0, x0 + n), V(x + "s", x0, x0 + n)]
        out = V("ps%d" % bank, 0, n)
        return run("P", vs, [out],
                   lambda: g.tensor.matmul_mx(ap(out), ap(vs[0]), ap(vs[1]), ap(vs[2]), ap(vs[3]), start, stop),
                   adds=not start)

    def ps(bank, a, b):
        return V("ps%d" % bank, a, b)

    def u8(v):
        return ap(v).bitcast(dt.uint8) if SCRATCH[v[0]][2] == X4 else ap(v)

    count["sent"] = 0

    def send(items):
        before("G", [it[2] for it in items], [])
        if len(items) == 1:
            dst, out, in_, sem, e = items[0]
            rid, pid = topo.addr(dst, core)
            g.remote_dma(u8(out), u8(in_), T.sem[sem], T.sem.sent, pid, rid, bits(e))
        else:
            trs = []
            for dst, out, in_, sem, e in items:
                rid, pid = topo.addr(dst, core)
                trs.append(RemoteDMATransfer(dst_ids=[DstId(rid=rid, pnc=pid)], dma_engine_mask=bits(e),
                                             remote_sem=T.sem[sem], src=u8(in_), dst=u8(out)))
            g.remote_dma_fused(trs, local_sem=T.sem.sent)
        count["sent"] += sum(len(it[4]) for it in items)

    eng = topo.engines(core, ha)
    q4 = len(eng) // 4
    off = topo.engines(core, p3)
    nfar = len(topo.engines(ha, p1))

    def swap_wide(src, land, sem):
        send([(ha, V(land + "c"), V(src + "c", 0, 52), sem, eng[q4:2 * q4]),
              (hc, V(land + "c"), V(src + "c", 52, 104), sem, eng[2 * q4:3 * q4]),
              (hb, V(land + "s"), V(src + "s"), sem, eng[3 * q4:])])

    def swap_narrow(src, land, sem):
        send([(ha, V(land + "c"), V(src + "c", 0, 52), sem, eng[:2 * q4]),
              (hb, V(land + "s"), V(src + "s"), sem, eng[2 * q4:])])

    def send2(dst, dst2, src, a, land, m, sem):
        send([(dst, V(land + "c"), V(src + "c", a, a + m), sem, eng[2 * q4:])])
        send([(dst2, V(land + "s"), V(src + "s", a, a + m), sem, eng[:2 * q4])])

    def mxv(name, a, b):
        return [V(name + "c", a, b), V(name + "s", a, b)]

    lands("a0", 3 * nfar, mxv("mid0", 8, 112))
    lands("a1", 2 * nfar, mxv("mid1", 12, 64))
    lands("a2", 2 * nfar, mxv("up1", 8, 60))
    lands("a3", len(off), mxv("up1", 60, 112))
    lands("ae", 2 * nfar, mxv("qab", 8, 112))
    lands("ah", 2 * nfar, mxv("qh1", 12, 64))
    lands("al", nfar, [V("lst", 0, 13)])

    dma("A", T.uat[:], T.ua[:], [], [V("uat")])
    dma("S", T.xt[:, 0:832], T.x[:, 0:832], [], [V("xt", 0, 832)])
    dma("S", T.xt[:, 832:1664], T.x[:, 832:1664], [], [V("xt", 832, 1664)])

    def tails(l, ks):
        for k in ks:
            at, w, short = planes(26 >> l)[0][k]
            const(V("z%d" % l, 4 * (at + short), 4 * (at + w)))

    iota(col("ci", 0), [[0, 1]], 0, 1)
    iota(V("eq"), [[0, 27], [1, 16]])
    iota(V("ci", 8, 16), [[16, 8]])
    iota(V("ident"), [[1, 128]])
    iota(V("gi"), [[1, 8], [0, 16]])
    tails(0, (0, 2, 3, 1, 4, 5, 6))
    const(V("kr"), 1)
    const(V("kr", 0, None, 16))
    fill(V("et", 0, 512), 0.0)
    ts(col("ci", 1), col("ci", 0), 15, ALU.bitwise_and)
    ts(col("ci", 2), col("ci", 0), 4, ALU.arith_shift_right)
    ts(col("ci", 3), col("ci", 0), 1, ALU.bitwise_and)
    ts(col("ci", 4), col("ci", 0), 4, ALU.arith_shift_right, 1, ALU.bitwise_and)
    ts(col("ci", 5), col("ci", 0), 2, ALU.arith_shift_right, 3, ALU.bitwise_and)
    ts(col("ci", 6), col("ci", 0), 3, ALU.bitwise_and)
    fill(V("et", 512, 1024), 0.0)
    tcopy(V("cf", 0, 7), V("ci", 0, 7))
    PP, Q16, GRP, ODDP, ODDG, Q4, B4, EVENP, SEG, E16, QC, LA, LC, K0 = [col("cf", i) for i in range(14)]
    fill(V("et", 1024, 1536), 0.0)
    ts(V("eq"), V("eq"), Q16, ALU.is_equal)
    tcopy(V("uof"), V("ci", 8, 16))
    fill(V("et", 1536, 2048), 0.0)

    def pick_codes(q, p):
        src, dst, lst = V(q + "c"), V(p + "c"), V("uof")
        run("V", [src, lst], [dst], lambda: g.vector.tensor_copy(
            ap(dst).bitcast(dt.uint32), ap(src).bitcast(dt.uint32).indirect(ap(lst))))

    def pick_scales(q, p):
        act(V(p + "s"), (V(q + "s"), V("uof")), ACT.Copy)

    act(K0, col("eq", 0), ACT.Identity, bias=2.0 * BIG, scale=-5.0 * BIG)
    act(V("k1"), V("eq", 0, C), ACT.Copy, scale=-3.0 * BIG)
    act(V("km"), V("eq", 0, C), ACT.Identity, bias=-BIG, scale=2.0 * BIG)
    act(V("k1", 0, None, 16), V("eq", 0, 26), ACT.Identity, bias=K0, scale=0.0)
    ts(V("ident"), V("ident"), PP, ALU.is_equal)
    quant("qa", 0, "uat", 0, 128)
    pick_scales("qa", "pa_")
    for b in range(4):
        act(V("et", 512 * b + b, 512 * b + 512, 4), V("ident"), ACT.Copy)
    pick_codes("qa", "pa_")
    for b in range(4):
        ts(V("gst", b, None, 4), V("gi"), GRP, ALU.is_equal, -1.0, ALU.mult)
    act(V("kc"), V("eq", 1, C + 1), ACT.Identity, bias=STEP, scale=-(DROP + STEP))
    act(QC, Q16, ACT.Copy, scale=STEP + 1.0)
    quant("qx", 0, "xt", 0, 208)
    quant("qg", 0, "gst", 0, 128)
    quant("qx", 208, "xt", 208, 208)
    quant("qe", 0, "et", 0, 512)
    const(col("jk", JW - 1))
    iota(V("cnt", 0, 26), [[-16, 26]], int(C - 16 - LOW - 15 * STEP))
    iota(V("k4"), [[0, 104], [1, 4]])
    iota(V("jv"), [[1, C]])
    const(V("lot", C, 512))
    const(V("let", C, 512))
    before("S", [V("xt")], [])
    dma("S", T.ubt[:], T.ub[:], [], [V("ubt")])
    dma("S", T.qwc[:].bitcast(dt.uint8), T.wc[:], [], [V("qwc")])
    dma("S", T.qws[:], T.ws[:], [], [V("qws")])
    dma("S", T.vt[:], T.v[:], [], [V("vt")])

    def orders(l, state_, scorer_):
        n = C >> l
        nb = n // 16
        nv = nb - 1 - ON_SCALAR[l]
        z, qz, dw = "z%d" % l, "qz%d" % l, "dw%d" % l
        pl = planes(nb)[0]
        mm(0, scorer_, 0, state_, 0, n)
        mm(1, scorer_, 0, state_, 0, n)
        for b in range(4):
            mm(4 + b, "qe", 128 * b, state_, 0, n)

        def flags(u, a, e):
            i = nb - u
            at = 4 * pl[i // 4][0] + i % 4
            return V(z, at + 4 * a, at + 4 * e - 3, 4)

        def own(u):
            return col("own", 16 * u + 15)

        def owned(a, e):
            scan(V("own", a, e), V("k1", a, e), V("dm", a, e), ALU.add, ALU.max)

        def masked(a, e):
            tt(V("dm", a, e), ps(0, a, e), V("km", a, e), ALU.min)

        hi, mid = CUTS[l]
        masked(hi, n)
        masked(mid, hi)
        owned(hi, n)
        masked(0, mid)
        owned(mid, hi)
        owned(0, mid)
        later = []
        for i, u in enumerate(range(nb - 1, nv, -1)):
            sg = V("sg", C * (i % 4), C * (i % 4) + 16 * u)
            act(sg, ps(1, 0, 16 * u), ACT.Sign, bias=own(u), scale=-1.0)
            if later:
                act(*later.pop())
            later.append((flags(u, 0, 16 * u), sg, ACT.Sign, 1.0, -1.0, col("rs", u)))
        act(*later.pop())
        for b in range(4):
            act(V(dw, b, 4 * n, 4), ps(4 + b, 0, n), ACT.Copy, scale=0.5)
        done, queued = [], []

        def plane(k):
            quant(qz, pl[k][0], z, pl[k][0], pl[k][1])
            queued.append(k)
            while queued and (done or 0 in queued):
                j = queued.pop(queued.index(0) if 0 in queued else 0)
                done.append(j)
                mm(2, "qg", 0, qz, pl[j][0], pl[j][1], len(done) == 1, len(done) == len(pl))

        mixed = [k for k in range(len(pl)) if nb - 4 * k > nv]
        for i, u in enumerate(range(nv, -LAG, -1)):
            if u > 0:
                ts(flags(u, 0, 16 * u), ps(0, 0, 16 * u), own(u), ALU.is_ge)
            if i == 0:
                tt(flags(nb, 0, n), ps(0, 0, n), V("own", 0, n), ALU.is_gt)
            if u == 5:
                scan(V("rd", 0, n), V("kr", 0, n), flags(nb, 0, n), ALU.mult, ALU.add)
                if l == 0:
                    ts(V("cnt", 0, 26), V("cnt", 0, 26), QC, ALU.add)
            if u == 1:
                tt(V("rr", 0, nb), V("rd", 15, n, 16), V("cnt", 26 - nb, 26), ALU.add)
            if i >= LAG:
                v = u + LAG
                e = (v + 1) * JW
                scan(V("jk", e - 8 * v, e), flags(v, 0, 8 * v), flags(v, 8 * v, 16 * v), ALU.add, ALU.add)
                k = (nb - v) // 4
                if k not in mixed and ((nb - v) % 4 == 3 or v == 1):
                    plane(k)
            for k, at in QUANT_AT[l].items():
                if at == i:
                    plane(k)
        for k in mixed:
            if k not in QUANT_AT[l]:
                plane(k)
        tt(V("kc", 15, 16 * (nv + 1), 16), V("jk", JW - 1, (nv + 1) * JW, JW), V("rr", 0, nv + 1), ALU.add)
        tt(V("kc", 16 * (nv + 1) + 15, n, 16), V("rs", nv + 1, nb), V("rr", nv + 1, nb), ALU.add)
        spare()
        scan(V("xo", 0, n), ps(2, 0, n), V("kc", 0, n), ALU.max, ALU.add, -DROP)
        spare()
        pos = V("pos%d" % l, 0, nb)
        ts(pos, V("xo", 15, n, 16), LOW, ALU.add)
        ts(V("rw%d" % l, 0, nb), V("xo", 15, n, 16), LOW, ALU.add)
        spare()
        tcopy((V("o%d" % l), pos), V("jv", 0, n))
        spare()

    waiting = []

    def spare():
        if waiting:
            waiting.pop(0)()

    def picked(l, s):
        m = (104, 56)[l]
        scan(V("xl", m * s, m * s + m), V("k4", 0, m), V("o%d" % l, s, 4 * m, 4), ALU.add, ALU.max)

    def lists(l, s0):
        m = (104, 56)[l]
        ts(V("ll%d" % l, m // 4 * s0, m // 4 * (s0 + 2)), V("xl", m * s0 + 3, m * (s0 + 2), 4), 4.0, ALU.mult,
           LC, ALU.add)

    def member(l, s, a, e):
        k = (26, 14)[l] * s
        return (V("dw%d" % l), V("ll%d" % l, k + a // 16, k + e // 16))

    def second(l, odd, a, e):
        return V("g%d" % l, (C >> l) * odd + a, (C >> l) * odd + e)

    def pairs(l, odd, tile, first, op, a=0, e=None):
        e = C >> l if e is None else e
        tt(V(tile, first + a, first + e), member(l, 2 * odd, a, e), second(l, odd, a, e), op)

    def odd_lows(l):
        n = C >> l
        a = (128, 64)[l]
        picked(l, 3)
        picked(l, 2)
        picked(l, 1)
        lists(l, 2)
        picked(l, 0)
        act(second(l, 1, a, n), member(l, 3, a, n), ACT.Copy)
        tcopy(second(l, 1, 0, a), member(l, 3, 0, a))
        lists(l, 0)
        act(second(l, 0, 0, n), member(l, 1, 0, n), ACT.Copy)
        spare()
        pairs(l, 1, "lot", 0, ALU.add, 0, a)
        pairs(l, 1, "lot", 0, ALU.add, a, n)
        spare()

    def layer(src, a, m, tile, first, step, split):
        order, bank = ((2, 0, 3, 1), 4) if split else (range(4), 0)
        for b in order:
            mm(bank + b, "qw", 128 * b, src, a, 128)
        for b in order:
            out = V(tile, first + b, step * m, step)
            if split and b >= 2:
                ts(out, ps(bank + b, 0, m), 0.03125, ALU.mult)
            else:
                act(out, ps(bank + b, 0, m), ACT.Copy, scale=0.03125)

    def unpack(bank, src, a, n, order=range(4)):
        for b in order:
            mm(bank + b, "qe", 128 * b, src, a, n)

    def list_constants():
        ts(V("k4"), V("k4"), Q4, ALU.is_equal, -(DROP + STEP), ALU.mult)
        act(V("k4"), V("k4"), ACT.Identity, bias=STEP)
        act(LA, Q4, ACT.Identity, bias=-12.0 * STEP, scale=4.0 * STEP)
        act(E16, ODDG, ACT.Copy, scale=16.0)
        act(EVENP, ODDP, ACT.Identity, bias=1.0, scale=-1.0)
        act(LC, B4, ACT.Identity, bias=LA)
        act(SEG, ODDP, ACT.Identity, bias=-104.0, scale=-104.0)
        quant("s0", 80, "et", 0, 128)

    tails(1, range(4))
    const(V("o1", 208, 224))
    const(V("ret", 256, 512))
    const(V("rot", 256, 512))
    const(V("ht1", 208, 512))
    waiting += [list_constants,
                lambda: (quant("qb", 0, "ubt", 0, 128), pick_scales("qb", "pb_")),
                lambda: quant("s1", 80, "et", 0, 128),
                lambda: pick_codes("qb", "pb_"),
                lambda: (ts(V("la", 0, 26), V("rw0", 0, 26), 1, ALU.arith_shift_right),
                         ts(V("la", 32, 58), V("rw0", 0, 26), 5, ALU.arith_shift_right)),
                lambda: pairs(0, 1, "ht0", C, ALU.subtract, 0, 96)]
    orders(0, "qx", "pa_")
    odd_lows(0)
    quant("s0", 0, "lot", 0, 128)
    swap_wide("s0", "r0", "h0")
    dma("S", T.ol[:, 0:C], T.o0[0:128:16, :], [V("o0")], [])
    const(V("ht1", 720, 1024))
    const(V("abe", C, 512))
    const(V("xb"))
    const(V("k32"), 1)
    const(V("k32", 0, None, 32))
    pairs(0, 0, "let", 0, ALU.add)
    ts(V("la", 64, 90), V("la", 32, 58), 16.0, ALU.mult, E16, ALU.add)
    quant("qv", 0, "vt", 0, 128)
    quant("mid0", 112, "let", 0, 128)
    layer("mid0", 112, 104, "at1", 0, 8, False)
    tt(V("la", 96, 122), V("la", 64, 90), V("la", 0, 26), ALU.add)
    pairs(0, 1, "ht0", C, ALU.subtract, 96, C)
    pairs(0, 0, "ht0", 0, ALU.subtract)
    tcopy(V("kk"), V("la", 96, 122))
    quant("s2", 80, "et", 0, 128)
    quant("qh0", 0, "ht0", 0, 208)
    layer("mid0", 8, 104, "at1", 4, 8, True)
    quant("qa1", 0, "at1", 0, 208)

    def signed(b):
        act(V("hs0", b, None, 4), (V("hw0", C * b, C * b + C), V("pos0")), ACT.Copy)

    def highs_by_place(bs):
        unpack(4, "qh0", 0, 208, bs)
        for b in bs:
            for h in range(2):
                for s in range(2):
                    act(V("hw0", C * b + 2 * h + s, C * b + C, 4), ps(4 + b, 104 * h, 104 * h + 104), ACT.Copy,
                        scale=1.0 - 2.0 * s)

    waiting += [lambda: highs_by_place(range(3)), lambda: 0, lambda: 0, lambda: ts(V("lb", 0, 13), V("rw1", 0, 13), EVENP, ALU.mult),
                lambda: 0, lambda: pairs(1, 1, "ht1", 0, ALU.subtract, 0, 96)]
    orders(1, "qa1", "pb_")
    send([(hd, V("rl", 0, 13), V("rw1", 0, 13), "hl", eng[:q4])])
    odd_lows(1)
    quant("s1", 0, "lot", 0, 128)
    swap_narrow("s1", "r1", "h1")
    dma("S", T.ol[:, C:C + 208], T.o1[0:128:16, 0:208], [V("o1")], [])
    highs_by_place((3,))
    signed(0)
    pairs(1, 0, "let", 0, ALU.add)
    pairs(1, 0, "ht1", 512, ALU.subtract, 0, 96)
    quant("mid1", 64, "let", 0, 128)
    layer("mid1", 64, 64, "ret", 0, 4, False)
    pairs(1, 0, "ht1", 512, ALU.subtract, 96, 208)
    pairs(1, 1, "ht1", 0, ALU.subtract, 96, 208)

    def highs(a, h, m):
        unpack(0, "qh1", a, 128)
        for b in range(4):
            act(V("hm", 156 * b + h, 156 * b + h + m), ps(b, 0, m), ACT.Copy)

    def put_back(src, h, tile, at):
        unpack(4, "up1", src, 128)
        for b in range(4):
            for s, op in enumerate((ALU.add, ALU.subtract)):
                tt(V(tile, at + 4 * s + b, at + C, 8), ps(4 + b, 0, 52), V("hm", 156 * b + h, 156 * b + h + 52), op)

    def table(bank, q0, a, order, split):
        unpack(bank, "qab", q0, 208, order)
        for b in order:
            out = V("dq", 4 * a + b, 4 * (a + 208), 4)
            if split and b >= 2:
                tcopy(out, ps(bank + b, 0, 208))
            else:
                act(out, ps(bank + b, 0, 208), ACT.Copy)

    both = V("lb", 32, 45)
    quant("qh1", 192, "ht1", 128, 128)
    highs(192, 0, 52)
    quant("up1", 112, "ret", 0, 128)
    quant("qh1", 64, "ht1", 0, 128)
    send2(hd, hc, "qh1", 64, "rh", 52, "hh")
    ts(V("lb", 16, 29), V("lst", 0, 13), ODDP, ALU.mult)
    put_back(112, 0, "abe", 0)
    tt(both, V("lb", 0, 13), V("lb", 16, 29), ALU.add)
    layer("mid1", 12, 64, "rot", 0, 4, False)
    quant("qab", 112, "abe", 0, 128)
    send2(hc, hd, "qab", 112, "re_", 104, "he")
    ts(V("lb", 48, 61), both, 2, ALU.arith_shift_right)
    ts(V("lb", 64, 77), both, 1, ALU.arith_shift_right, 1, ALU.bitwise_and)
    quant("s2", 0, "rot", 0, 128)
    swap_narrow("s2", "r2", "h2")
    send([(p3, V("up1c", 60, 112), V("s2c", 0, 52), "a3", off[:len(off) // 2])])
    send([(p3, V("up1s", 60, 112), V("s2s", 0, 52), "a3", off[len(off) // 2:])])
    signed(1)
    signed(2)
    ts(V("lb", 80, 93), V("lb", 48, 61), -2.0, ALU.mult, SEG, ALU.add)
    ts(V("lb", 96, 109), V("lb", 64, 77), 206.0, ALU.mult)
    tt(V("lb", 112, 125), both, V("lb", 80, 93), ALU.add)
    tt(V("xb", 0, None, 32), V("lb", 112, 125), V("lb", 96, 109), ALU.add)
    scan(V("rd"), V("k32"), V("xb"), ALU.mult, ALU.add)
    turn(V("tb"), V("rd"))
    highs(12, 52, 104)
    act(V("yt"), (V("tb"), V("kk")), ACT.Identity, bias=208.0)
    signed(3)
    put_back(60, 52, "abl", 0)
    put_back(8, 104, "abl", C)
    scan(V("xo"), V("k4"), V("yt"), ALU.add, ALU.max)
    quant("qab", 240, "abl", 0, 208)
    table(0, 8, 0, range(4), False)
    ts(V("lq"), V("xo", 3, None, 4), 4.0, ALU.mult, LC, ALU.add)
    table(4, 240, 208, (2, 0, 3, 1), True)

    parts = ((0, 144), (144, 288), (288, C))

    def gather(a, e):
        tt(V("u0t", 4 * a, 4 * e), (V("dq"), V("lq", a // 4, e // 4)), V("hs0", 4 * a, 4 * e), ALU.add)

    gather(*parts[0])
    for h, (a, e) in enumerate(parts):
        if h != 1:
            gather(*parts[max(h, 1)])
        quant("qu0", a, "u0t", a, e - a)
        mm(4 + h, "qv", 0, "qu0", a, e - a)
        dma("S", T.oc[:, 4 * a:4 * e], T.qu0c[:, a:e].bitcast(dt.uint8), [V("qu0c", a, e)], [])
        if h == len(parts) - 1:
            for k in range(4):
                dma("S" if k < 2 else "A", T.osc[4 * k:4 * k + 4, :], T.qu0s[32 * k:32 * k + 4, :], [V("qu0s")], [])
        act(V("yt", a, e), ps(4 + h, 0, e - a), ACT.Copy)
        dma("A" if h < len(parts) - 1 else "S", T.y[:, a:e], T.yt[:, a:e], [V("yt", a, e)], [])

    for sem, n in count.items():
        if clock["G"].get(sem, 0) < n:
            g.wait_ge(T.sem[sem], n)
